import numpy as np
import ml_dtypes


def mxq(x, axis, fmt="e4m3"):
    dtype, down = {"e4m3": (ml_dtypes.float8_e4m3fn, 7), "e5m2": (ml_dtypes.float8_e5m2, 14)}[fmt]
    v = np.moveaxis(np.asarray(x, np.float32).astype(ml_dtypes.bfloat16).astype(np.float64), axis, -1)
    blocks = v.reshape(v.shape[:-1] + (-1, 32))
    amax = np.abs(blocks).max(-1, keepdims=True)
    byte = np.maximum(np.where(amax > 0, np.frexp(amax)[1] - 1 + 127, 0) - down, 1)
    scale = np.exp2(byte - 127.0)
    codes = (blocks / scale).astype(np.float32).astype(dtype).astype(np.float64)
    return np.moveaxis((codes * scale).reshape(v.shape), -1, axis)


WIDE = False


def mx_kscale(k):
    if not WIDE:
        return np.ones(k)
    levels = np.array([10, -10, 5, -5, 0])
    if k % 512:
        return np.exp2(np.random.permutation(np.resize(levels, k // 32))).repeat(32)
    a = np.empty((k // 512, 16))
    for p in range(k // 512):
        a[p, :8] = np.random.permutation(np.resize(levels, 8))
        for g in range(8):
            far = levels[np.abs(levels - a[p, g]) >= 10]
            a[p, g + 8] = far[np.random.randint(len(far))]
    return np.exp2(a.ravel()).repeat(32)


def f64(x):
    return np.asarray(x).astype(np.float64)


def striped(idx):
    return np.tile(idx.reshape(-1, 16).T, (8, 1)).astype(np.uint16)


def unstriped(offs):
    return offs[:16].T.reshape(-1).astype(np.int64)


E2M1 = np.array([0.0, 0.5, 1.0, 1.5, 2.0, 3.0, 4.0, 6.0, -0.0, -0.5, -1.0, -1.5, -2.0, -3.0, -4.0, -6.0])


def pack_weight(w, fmt):
    k, n = w.shape
    w = f64(np.asarray(w, np.float32).astype(ml_dtypes.bfloat16)).reshape(k // 32, 32, n)
    amax = np.abs(w).max(1)
    if fmt == "e4m3":
        byte = np.frexp(amax)[1] - 1 + 127 - 7
    else:
        mant, ex = np.frexp(amax / 6.0)
        byte = np.where(mant > 0.5, ex, ex - 1) + 127
    byte = np.clip(np.where(amax > 0, byte, 1), 1, 254)
    scaled = (w * np.exp2(127.0 - byte)[:, None, :]).reshape(k, n).astype(np.float32)
    by_word = np.ascontiguousarray(scaled.reshape(k // 512, 128, 4, n).transpose(0, 1, 3, 2))
    if fmt == "e4m3":
        words = by_word.astype(ml_dtypes.float8_e4m3fn).view(np.uint8)
    else:
        c = by_word.astype(ml_dtypes.float4_e2m1fn).view(np.uint8) & 0xF
        words = (c[..., 0::2] | (c[..., 1::2] << 4)).reshape(k // 512, 128, 2 * n)
    return np.ascontiguousarray(words), np.ascontiguousarray(byte.astype(np.uint8).reshape(k // 512, 16, n))


def unpack_weight(words, scales, fmt):
    g, _, n = scales.shape
    words = np.ascontiguousarray(words).reshape(g, 128, n, -1)
    if fmt == "e4m3":
        vals = words.view(ml_dtypes.float8_e4m3fn).astype(np.float64)
    else:
        nib = np.empty((g, 128, n, 4), np.uint8)
        nib[..., 0::2] = words & 0xF
        nib[..., 1::2] = words >> 4
        vals = E2M1[nib]
    vals = vals * np.repeat(np.exp2(scales.astype(np.float64) - 127.0), 8, axis=1)[..., None]
    return vals.transpose(0, 1, 3, 2).reshape(g * 512, n)


K, M, T, S = 1024, 512, 4096, 2048


def setup_inputs():
    n = np.random.standard_normal
    s = mx_kscale(K)[:, None]
    v = pack_weight(n((K, T)) * s, "e4m3")
    return {
        "tab_words": v[0],
        "tab_scales": v[1],
        "w": (n((K, M)) / np.sqrt(K) / s).astype(np.float32),
        "gT": n((M, T)).astype(np.float32),
        "b": (0.3 * n(512)).astype(np.float32),
        "offs": striped(np.random.permutation(T)[:S]),
    }


def reference(tab_words, tab_scales, w, gT, b, offs):
    tab_ = unpack_weight(tab_words, tab_scales, "e4m3")[:, unstriped(offs)]
    w_ = mxq(f64(w), 0, "e4m3")
    y = w_.T @ tab_
    return (y + f64(b)[:, None]) * f64(gT)[:, unstriped(offs)]

@@ -1,0 +1,130 @@
+from contextlib import ExitStack
+
+import concourse.mybir as mybir
+
+K, M, T, S = 1024, 512, 4096, 2048
+FLOPS = 2 * K * M * S
+
+F32 = mybir.dt.float32
+BF16 = mybir.dt.bfloat16
+I32 = mybir.dt.int32
+U32 = mybir.dt.uint32
+U16 = mybir.dt.uint16
+U8 = mybir.dt.uint8
+FP8X4 = mybir.dt.float8_e4m3fn_x4
+IDENTITY = mybir.ActivationFunctionType.Identity
+MULT = mybir.AluOpType.mult
+
+P = 128
+PACK = 4
+K_PASS = P * PACK
+PASSES = K // K_PASS
+N_TILES = M // P
+BANK = 512
+HALF = S // 2
+LIST_ROWS = 16
+QUADRANT = 32
+SCALE_ROWS = 4
+
+
+def tile_list_tabgate_bias_kernel(tc, tab_words, tab_scales, w, gT, b, offs, out):
+    nc = tc.nc
+    with ExitStack() as ctx:
+        held = ctx.enter_context(tc.tile_pool(name="held", bufs=1))
+        psum = ctx.enter_context(tc.psum_pool(name="psum", bufs=8))
+
+        offsets = held.tile([P, S // LIST_ROWS], U16, name="offsets")
+        nc.sync.dma_start(offsets[:], offs)
+
+        def entries(j0, j1):
+            return offsets[:, j0 // LIST_ROWS : j1 // LIST_ROWS]
+
+        scale_table = held.tile([P, T], U8, name="scale_table", align_bytes=64)
+        nc.gpsimd.memset(scale_table[:].bitcast(I32), 0)
+        for q in range(P // QUADRANT):
+            rows = slice(QUADRANT * q, QUADRANT * q + PASSES * SCALE_ROWS)
+            nc.gpsimd.dma_start(
+                out=scale_table[rows, :].bitcast(I32),
+                in_=tab_scales[:, SCALE_ROWS * q : SCALE_ROWS * (q + 1), :].bitcast(I32),
+            )
+
+        w_raw = []
+        for a in range(PASSES):
+            raw = held.tile([P, PACK, M], F32, name="w_raw%d" % a)
+            nc.sync.dma_start(
+                out=raw[:], in_=w[a * K_PASS : (a + 1) * K_PASS, :].rearrange("(p i) n -> p i n", i=PACK)
+            )
+            w_raw.append(raw)
+        bias = held.tile([P, N_TILES], F32, name="bias")
+        nc.sync.dma_start(out=bias[:], in_=b.rearrange("(p t) -> p t", t=N_TILES))
+
+        word_table = []
+        for a in range(PASSES):
+            words = held.tile([P, T], I32, name="word_table%d" % a, align_bytes=64)
+            nc.sync.dma_start(out=words[:], in_=tab_words[a].rearrange("p c i -> p (c i)").bitcast(I32))
+            word_table.append(words)
+
+        gT_rows = gT.rearrange("(p t) c -> t p c", t=N_TILES)
+        out_rows = out.rearrange("(p t) j -> t p j", t=N_TILES)
+        gate_table = []
+        for t in range(N_TILES):
+            gates = held.tile([P, T], F32, name="gate_table%d" % t, align_bytes=64)
+            nc.sync.dma_start(out=gates[:], in_=gT_rows[t])
+            gate_table.append(gates)
+
+        v_scales = held.tile([P, S], U8, name="v_scales", align_bytes=64)
+        nc.vector.tensor_copy(v_scales[:], scale_table[:].indirect(offsets[:]))
+
+        w_codes, w_scales = [], []
+        for a in range(PASSES):
+            grouped = held.tile([P, M * PACK], BF16, name="w_grouped%d" % a, align_bytes=64)
+            nc.scalar.copy(
+                out=grouped[:].rearrange("p (t m i) -> p m t i", t=N_TILES, i=PACK),
+                in_=w_raw[a][:].rearrange("p i (m t) -> p m t i", t=N_TILES),
+            )
+            codes = held.tile([P, M], U32, name="w_codes%d" % a, align_bytes=64)
+            scales = held.tile([P, M], U8, name="w_scales%d" % a, align_bytes=64)
+            nc.vector.quantize_mx(out=codes[:].bitcast(FP8X4), scales=scales[:], in_=grouped[:])
+            w_codes.append(codes)
+            w_scales.append(scales)
+
+        first = held.tile([P, S], U32, name="v_codes0", align_bytes=64)
+        nc.vector.tensor_copy(first[:], word_table[0][:].bitcast(U32).indirect(offsets[:]))
+        v_codes = [[first[:, 0:HALF], first[:, HALF:S]], []]
+        for h in range(2):
+            picked = held.tile([P, HALF], U32, name="v_codes1_%d" % h, align_bytes=64)
+            nc.vector.tensor_copy(
+                picked[:], word_table[1][:].bitcast(U32).indirect(entries(h * HALF, (h + 1) * HALF))
+            )
+            v_codes[1].append(picked[:])
+
+        for t in range(N_TILES):
+            t_cols = slice(t * P, (t + 1) * P)
+            biased = held.tile([P, S], F32, name="biased%d" % t)
+            for j0 in range(0, S, BANK):
+                h, c0 = divmod(j0, HALF)
+                acc = psum.tile([P, BANK], F32, name="acc")
+                for a in range(PASSES):
+                    nc.tensor.matmul_mx(
+                        out=acc[:],
+                        lhsT=w_codes[a][:, t_cols].bitcast(FP8X4),
+                        lhsT_scale=w_scales[a][:, t_cols],
+                        rhs=v_codes[a][h][:, c0 : c0 + BANK].bitcast(FP8X4),
+                        rhs_scale=v_scales[SCALE_ROWS * a : P, j0 : j0 + BANK],
+                        start=(a == 0),
+                        stop=(a == PASSES - 1),
+                    )
+                nc.scalar.activation(
+                    out=biased[:, j0 : j0 + BANK], in_=acc[:], func=IDENTITY, bias=bias[:, t : t + 1]
+                )
+            result = held.tile([P, S], F32, name="result%d" % t)
+            width = HALF if t in (0, N_TILES - 1) else S
+            for j0 in range(0, S, width):
+                cols = slice(j0, j0 + width)
+                nc.vector.tensor_tensor(
+                    result[:, cols], gate_table[t][:].indirect(entries(j0, j0 + width)), biased[:, cols], MULT
+                )
+                if t == N_TILES - 1:
+                    nc.sync.dma_start(out=out_rows[t][:, cols], in_=result[:, cols])
+            if t < N_TILES - 1:
+                nc.sync.dma_start(out=out_rows[t], in_=result[:])

@@ -25,13 +25,15 @@ HALF = S // 2
 LIST_ROWS = 16
 QUADRANT = 32
 SCALE_ROWS = 4
+BANKS = 6
+LEAD = 512
 
 
 def tile_list_tabgate_bias_kernel(tc, tab_words, tab_scales, w, gT, b, offs, out):
     nc = tc.nc
     with ExitStack() as ctx:
         held = ctx.enter_context(tc.tile_pool(name="held", bufs=1))
-        psum = ctx.enter_context(tc.psum_pool(name="psum", bufs=8))
+        psum = ctx.enter_context(tc.psum_pool(name="psum", bufs=BANKS))
 
         offsets = held.tile([P, S // LIST_ROWS], U16, name="offsets")
         nc.sync.dma_start(offsets[:], offs)
@@ -39,14 +41,26 @@ def tile_list_tabgate_bias_kernel(tc, tab_words, tab_scales, w, gT, b, offs, out
         def entries(j0, j1):
             return offsets[:, j0 // LIST_ROWS : j1 // LIST_ROWS]
 
+        bias = held.tile([P, N_TILES], F32, name="bias")
+        nc.sync.dma_start(out=bias[:], in_=b.rearrange("(p t) -> p t", t=N_TILES))
+
+        word_table = [held.tile([P, T], I32, name="word_table%d" % a, align_bytes=64) for a in range(PASSES)]
+
+        def load_words(a, c0, c1):
+            rows = tab_words[a].rearrange("p c i -> p (c i)").bitcast(I32)
+            nc.sync.dma_start(out=word_table[a][:, c0:c1], in_=rows[:, c0:c1])
+
         scale_table = held.tile([P, T], U8, name="scale_table", align_bytes=64)
-        nc.gpsimd.memset(scale_table[:].bitcast(I32), 0)
+        nc.vector.memset(scale_table[:].bitcast(I32), 0)
+        load_words(0, 0, LEAD)
+        load_words(0, LEAD, 2 * LEAD)
         for q in range(P // QUADRANT):
             rows = slice(QUADRANT * q, QUADRANT * q + PASSES * SCALE_ROWS)
-            nc.gpsimd.dma_start(
+            nc.sync.dma_start(
                 out=scale_table[rows, :].bitcast(I32),
                 in_=tab_scales[:, SCALE_ROWS * q : SCALE_ROWS * (q + 1), :].bitcast(I32),
             )
+        load_words(0, 2 * LEAD, T)
 
         w_raw = []
         for a in range(PASSES):
@@ -55,14 +69,8 @@ def tile_list_tabgate_bias_kernel(tc, tab_words, tab_scales, w, gT, b, offs, out
                 out=raw[:], in_=w[a * K_PASS : (a + 1) * K_PASS, :].rearrange("(p i) n -> p i n", i=PACK)
             )
             w_raw.append(raw)
-        bias = held.tile([P, N_TILES], F32, name="bias")
-        nc.sync.dma_start(out=bias[:], in_=b.rearrange("(p t) -> p t", t=N_TILES))
 
-        word_table = []
-        for a in range(PASSES):
-            words = held.tile([P, T], I32, name="word_table%d" % a, align_bytes=64)
-            nc.sync.dma_start(out=words[:], in_=tab_words[a].rearrange("p c i -> p (c i)").bitcast(I32))
-            word_table.append(words)
+        load_words(1, 0, T)
 
         gT_rows = gT.rearrange("(p t) c -> t p c", t=N_TILES)
         out_rows = out.rearrange("(p t) j -> t p j", t=N_TILES)
@@ -74,6 +82,8 @@ def tile_list_tabgate_bias_kernel(tc, tab_words, tab_scales, w, gT, b, offs, out
 
         v_scales = held.tile([P, S], U8, name="v_scales", align_bytes=64)
         nc.vector.tensor_copy(v_scales[:], scale_table[:].indirect(offsets[:]))
+        first_words = held.tile([P, S], U32, name="first_words", align_bytes=64)
+        nc.vector.tensor_copy(first_words[:], word_table[0][:].bitcast(U32).indirect(offsets[:]))
 
         w_codes, w_scales = [], []
         for a in range(PASSES):
@@ -88,15 +98,13 @@ def tile_list_tabgate_bias_kernel(tc, tab_words, tab_scales, w, gT, b, offs, out
             w_codes.append(codes)
             w_scales.append(scales)
 
-        first = held.tile([P, S], U32, name="v_codes0", align_bytes=64)
-        nc.vector.tensor_copy(first[:], word_table[0][:].bitcast(U32).indirect(offsets[:]))
-        v_codes = [[first[:, 0:HALF], first[:, HALF:S]], []]
-        for h in range(2):
-            picked = held.tile([P, HALF], U32, name="v_codes1_%d" % h, align_bytes=64)
+        v_words = [[first_words[:, 0:HALF], first_words[:, HALF:S]], []]
+        for h in range(S // HALF):
+            picked = held.tile([P, HALF], U32, name="second_words%d" % h, align_bytes=64)
             nc.vector.tensor_copy(
                 picked[:], word_table[1][:].bitcast(U32).indirect(entries(h * HALF, (h + 1) * HALF))
             )
-            v_codes[1].append(picked[:])
+            v_words[1].append(picked[:])
 
         for t in range(N_TILES):
             t_cols = slice(t * P, (t + 1) * P)
@@ -109,7 +117,7 @@ def tile_list_tabgate_bias_kernel(tc, tab_words, tab_scales, w, gT, b, offs, out
                         out=acc[:],
                         lhsT=w_codes[a][:, t_cols].bitcast(FP8X4),
                         lhsT_scale=w_scales[a][:, t_cols],
-                        rhs=v_codes[a][h][:, c0 : c0 + BANK].bitcast(FP8X4),
+                        rhs=v_words[a][h][:, c0 : c0 + BANK].bitcast(FP8X4),
                         rhs_scale=v_scales[SCALE_ROWS * a : P, j0 : j0 + BANK],
                         start=(a == 0),
                         stop=(a == PASSES - 1),
@@ -117,14 +125,21 @@ def tile_list_tabgate_bias_kernel(tc, tab_words, tab_scales, w, gT, b, offs, out
                 nc.scalar.activation(
                     out=biased[:, j0 : j0 + BANK], in_=acc[:], func=IDENTITY, bias=bias[:, t : t + 1]
                 )
+
+            last = t == N_TILES - 1
+            if last:
+                cuts = [0, HALF, HALF + BANK, S]
+            elif t < N_TILES // 2:
+                cuts = [0, HALF, S]
+            else:
+                cuts = [0, S]
             result = held.tile([P, S], F32, name="result%d" % t)
-            width = HALF if t in (0, N_TILES - 1) else S
-            for j0 in range(0, S, width):
-                cols = slice(j0, j0 + width)
+            for j0, j1 in zip(cuts, cuts[1:]):
+                cols = slice(j0, j1)
                 nc.vector.tensor_tensor(
-                    result[:, cols], gate_table[t][:].indirect(entries(j0, j0 + width)), biased[:, cols], MULT
+                    result[:, cols], gate_table[t][:].indirect(entries(j0, j1)), biased[:, cols], MULT
                 )
-                if t == N_TILES - 1:
+                if last:
                     nc.sync.dma_start(out=out_rows[t][:, cols], in_=result[:, cols])
-            if t < N_TILES - 1:
+            if not last:
                 nc.sync.dma_start(out=out_rows[t], in_=result[:])

@@ -27,6 +27,7 @@ QUADRANT = 32
 SCALE_ROWS = 4
 BANKS = 6
 LEAD = 512
+LAST_CUT = 1408
 
 
 def tile_list_tabgate_bias_kernel(tc, tab_words, tab_scales, w, gT, b, offs, out):
@@ -54,7 +55,7 @@ def tile_list_tabgate_bias_kernel(tc, tab_words, tab_scales, w, gT, b, offs, out
         nc.vector.memset(scale_table[:].bitcast(I32), 0)
         load_words(0, 0, LEAD)
         load_words(0, LEAD, 2 * LEAD)
-        for q in range(P // QUADRANT):
+        for q in (2, 3, 0, 1):
             rows = slice(QUADRANT * q, QUADRANT * q + PASSES * SCALE_ROWS)
             nc.sync.dma_start(
                 out=scale_table[rows, :].bitcast(I32),
@@ -73,7 +74,7 @@ def tile_list_tabgate_bias_kernel(tc, tab_words, tab_scales, w, gT, b, offs, out
         load_words(1, 0, T)
 
         gT_rows = gT.rearrange("(p t) c -> t p c", t=N_TILES)
-        out_rows = out.rearrange("(p t) j -> t p j", t=N_TILES)
+        out_rows = out.rearrange("(p t) j -> p (t j)", t=N_TILES)
         gate_table = []
         for t in range(N_TILES):
             gates = held.tile([P, T], F32, name="gate_table%d" % t, align_bytes=64)
@@ -106,6 +107,9 @@ def tile_list_tabgate_bias_kernel(tc, tab_words, tab_scales, w, gT, b, offs, out
             )
             v_words[1].append(picked[:])
 
+        result = held.tile([P, N_TILES * S], F32, name="result")
+        store_ends = [2 * S, 3 * S, 3 * S + LAST_CUT, 4 * S]
+        stored = 0
         for t in range(N_TILES):
             t_cols = slice(t * P, (t + 1) * P)
             biased = held.tile([P, S], F32, name="biased%d" % t)
@@ -126,20 +130,21 @@ def tile_list_tabgate_bias_kernel(tc, tab_words, tab_scales, w, gT, b, offs, out
                     out=biased[:, j0 : j0 + BANK], in_=acc[:], func=IDENTITY, bias=bias[:, t : t + 1]
                 )
 
-            last = t == N_TILES - 1
-            if last:
-                cuts = [0, HALF, HALF + BANK, S]
-            elif t < N_TILES // 2:
+            if t == 0:
                 cuts = [0, HALF, S]
+            elif t == N_TILES - 1:
+                cuts = [0, LAST_CUT, S]
             else:
                 cuts = [0, S]
-            result = held.tile([P, S], F32, name="result%d" % t)
             for j0, j1 in zip(cuts, cuts[1:]):
-                cols = slice(j0, j1)
+                done = t * S + j1
                 nc.vector.tensor_tensor(
-                    result[:, cols], gate_table[t][:].indirect(entries(j0, j1)), biased[:, cols], MULT
+                    result[:, t * S + j0 : done],
+                    gate_table[t][:].indirect(entries(j0, j1)),
+                    biased[:, j0:j1],
+                    MULT,
                 )
-                if last:
-                    nc.sync.dma_start(out=out_rows[t][:, cols], in_=result[:, cols])
-            if not last:
-                nc.sync.dma_start(out=out_rows[t], in_=result[:])
+                if done in store_ends:
+                    cols = slice(stored, done)
+                    nc.sync.dma_start(out=out_rows[:, cols], in_=result[:, cols])
+                    stored = done

@@ -26,7 +26,7 @@ LIST_ROWS = 16
 QUADRANT = 32
 SCALE_ROWS = 4
 BANKS = 6
-LEAD = 512
+WINDOW = 4 * T
 LAST_CUT = 1408
 
 
@@ -34,6 +34,7 @@ def tile_list_tabgate_bias_kernel(tc, tab_words, tab_scales, w, gT, b, offs, out
     nc = tc.nc
     with ExitStack() as ctx:
         held = ctx.enter_context(tc.tile_pool(name="held", bufs=1))
+        late = ctx.enter_context(tc.tile_pool(name="late", bufs=1))
         psum = ctx.enter_context(tc.psum_pool(name="psum", bufs=BANKS))
 
         offsets = held.tile([P, S // LIST_ROWS], U16, name="offsets")
@@ -45,23 +46,20 @@ def tile_list_tabgate_bias_kernel(tc, tab_words, tab_scales, w, gT, b, offs, out
         bias = held.tile([P, N_TILES], F32, name="bias")
         nc.sync.dma_start(out=bias[:], in_=b.rearrange("(p t) -> p t", t=N_TILES))
 
-        word_table = [held.tile([P, T], I32, name="word_table%d" % a, align_bytes=64) for a in range(PASSES)]
+        scale_table = late.tile([P, T], U8, name="scale_table", offset=WINDOW - T // 2, align_bytes=64)
+        nc.sync.dma_start(
+            out=scale_table[0:QUADRANT, :].bitcast(I32), in_=tab_scales.rearrange("a q c -> (a q) c").bitcast(I32)
+        )
+        nc.vector.memset(scale_table[QUADRANT : 2 * QUADRANT, :].bitcast(I32), 0)
+        nc.vector.memset(scale_table[2 * QUADRANT : P, :].bitcast(I32), 0)
+        v_scales = held.tile([P, S], U8, name="v_scales", align_bytes=64)
+        nc.vector.memset(v_scales[:].bitcast(I32), 0)
 
-        def load_words(a, c0, c1):
-            rows = tab_words[a].rearrange("p c i -> p (c i)").bitcast(I32)
-            nc.sync.dma_start(out=word_table[a][:, c0:c1], in_=rows[:, c0:c1])
+        def load_words(a, words):
+            nc.sync.dma_start(out=words[:], in_=tab_words[a].rearrange("p c i -> p (c i)").bitcast(I32))
 
-        scale_table = held.tile([P, T], U8, name="scale_table", align_bytes=64)
-        nc.vector.memset(scale_table[:].bitcast(I32), 0)
-        load_words(0, 0, LEAD)
-        load_words(0, LEAD, 2 * LEAD)
-        for q in (2, 3, 0, 1):
-            rows = slice(QUADRANT * q, QUADRANT * q + PASSES * SCALE_ROWS)
-            nc.sync.dma_start(
-                out=scale_table[rows, :].bitcast(I32),
-                in_=tab_scales[:, SCALE_ROWS * q : SCALE_ROWS * (q + 1), :].bitcast(I32),
-            )
-        load_words(0, 2 * LEAD, T)
+        word_table = [late.tile([P, T], I32, name="word_table0", offset=4 * WINDOW, align_bytes=64)]
+        load_words(0, word_table[0])
 
         w_raw = []
         for a in range(PASSES):
@@ -71,20 +69,30 @@ def tile_list_tabgate_bias_kernel(tc, tab_words, tab_scales, w, gT, b, offs, out
             )
             w_raw.append(raw)
 
-        load_words(1, 0, T)
+        picked_scales = late.tile([P, S], U8, name="picked_scales", offset=3 * WINDOW - S // 2, align_bytes=64)
+        nc.vector.tensor_copy(picked_scales[:], scale_table[:].indirect(offsets[:]))
+        first_words = held.tile([P, S], U32, name="first_words", align_bytes=64)
+        nc.vector.tensor_copy(first_words[:], word_table[0][:].bitcast(U32).indirect(offsets[:]))
+
+        def place_scales(a):
+            for r in range(SCALE_ROWS):
+                nc.sync.dma_start(
+                    out=v_scales[SCALE_ROWS * a + r : P : QUADRANT, :].bitcast(I32),
+                    in_=picked_scales[16 * a + r : 16 * (a + 1) : SCALE_ROWS, :].bitcast(I32),
+                )
+
+        place_scales(0)
+        word_table.append(late.tile([P, T], I32, name="word_table1", offset=0, align_bytes=64))
+        load_words(1, word_table[1])
+        place_scales(1)
 
         gT_rows = gT.rearrange("(p t) c -> t p c", t=N_TILES)
         out_rows = out.rearrange("(p t) j -> p (t j)", t=N_TILES)
         gate_table = []
-        for t in range(N_TILES):
-            gates = held.tile([P, T], F32, name="gate_table%d" % t, align_bytes=64)
+        for t, slot in enumerate((1, 4, 2, 3)):
+            gates = late.tile([P, T], F32, name="gate_table%d" % t, offset=slot * WINDOW, align_bytes=64)
             nc.sync.dma_start(out=gates[:], in_=gT_rows[t])
             gate_table.append(gates)
-
-        v_scales = held.tile([P, S], U8, name="v_scales", align_bytes=64)
-        nc.vector.tensor_copy(v_scales[:], scale_table[:].indirect(offsets[:]))
-        first_words = held.tile([P, S], U32, name="first_words", align_bytes=64)
-        nc.vector.tensor_copy(first_words[:], word_table[0][:].bitcast(U32).indirect(offsets[:]))
 
         w_codes, w_scales = [], []
         for a in range(PASSES):

@@ -74,17 +74,18 @@ def tile_list_tabgate_bias_kernel(tc, tab_words, tab_scales, w, gT, b, offs, out
         first_words = held.tile([P, S], U32, name="first_words", align_bytes=64)
         nc.vector.tensor_copy(first_words[:], word_table[0][:].bitcast(U32).indirect(offsets[:]))
 
-        def place_scales(a):
-            for r in range(SCALE_ROWS):
-                nc.sync.dma_start(
-                    out=v_scales[SCALE_ROWS * a + r : P : QUADRANT, :].bitcast(I32),
-                    in_=picked_scales[16 * a + r : 16 * (a + 1) : SCALE_ROWS, :].bitcast(I32),
-                )
+        def place_scales(rows):
+            for r in rows:
+                for a in range(PASSES):
+                    nc.sync.dma_start(
+                        out=v_scales[SCALE_ROWS * a + r : P : QUADRANT, :].bitcast(I32),
+                        in_=picked_scales[16 * a + r : 16 * (a + 1) : SCALE_ROWS, :].bitcast(I32),
+                    )
 
-        place_scales(0)
+        place_scales((0, 1))
         word_table.append(late.tile([P, T], I32, name="word_table1", offset=0, align_bytes=64))
         load_words(1, word_table[1])
-        place_scales(1)
+        place_scales((2, 3))
 
         gT_rows = gT.rearrange("(p t) c -> t p c", t=N_TILES)
         out_rows = out.rearrange("(p t) j -> p (t j)", t=N_TILES)

@@ -25,7 +25,7 @@ HALF = S // 2
 LIST_ROWS = 16
 QUADRANT = 32
 SCALE_ROWS = 4
-BANKS = 6
+BANKS = 4
 WINDOW = 4 * T
 LAST_CUT = 1408
 
@@ -46,7 +46,7 @@ def tile_list_tabgate_bias_kernel(tc, tab_words, tab_scales, w, gT, b, offs, out
         bias = held.tile([P, N_TILES], F32, name="bias")
         nc.sync.dma_start(out=bias[:], in_=b.rearrange("(p t) -> p t", t=N_TILES))
 
-        scale_table = late.tile([P, T], U8, name="scale_table", offset=WINDOW - T // 2, align_bytes=64)
+        scale_table = late.tile([P, T], U8, name="scale_table", offset=WINDOW // 2 - T // 2, align_bytes=64)
         nc.sync.dma_start(
             out=scale_table[0:QUADRANT, :].bitcast(I32), in_=tab_scales.rearrange("a q c -> (a q) c").bitcast(I32)
         )
@@ -58,18 +58,20 @@ def tile_list_tabgate_bias_kernel(tc, tab_words, tab_scales, w, gT, b, offs, out
         def load_words(a, words):
             nc.sync.dma_start(out=words[:], in_=tab_words[a].rearrange("p c i -> p (c i)").bitcast(I32))
 
-        word_table = [late.tile([P, T], I32, name="word_table0", offset=4 * WINDOW, align_bytes=64)]
+        word_table = [late.tile([P, T], I32, name="word_table0", offset=2 * WINDOW, align_bytes=64)]
         load_words(0, word_table[0])
 
-        w_raw = []
-        for a in range(PASSES):
-            raw = held.tile([P, PACK, M], F32, name="w_raw%d" % a)
+        def load_w(a, raw):
             nc.sync.dma_start(
                 out=raw[:], in_=w[a * K_PASS : (a + 1) * K_PASS, :].rearrange("(p i) n -> p i n", i=PACK)
             )
-            w_raw.append(raw)
 
-        picked_scales = late.tile([P, S], U8, name="picked_scales", offset=3 * WINDOW - S // 2, align_bytes=64)
+        w_raw = [held.tile([P, PACK, M], F32, name="w_raw0")]
+        load_w(0, w_raw[0])
+        word_table.append(held.tile([P, T], I32, name="word_table1", align_bytes=64))
+        load_words(1, word_table[1])
+
+        picked_scales = late.tile([P, S], U8, name="picked_scales", offset=9 * WINDOW // 2 - S, align_bytes=64)
         nc.vector.tensor_copy(picked_scales[:], scale_table[:].indirect(offsets[:]))
         first_words = held.tile([P, S], U32, name="first_words", align_bytes=64)
         nc.vector.tensor_copy(first_words[:], word_table[0][:].bitcast(U32).indirect(offsets[:]))
@@ -83,60 +85,60 @@ def tile_list_tabgate_bias_kernel(tc, tab_words, tab_scales, w, gT, b, offs, out
                     )
 
         place_scales((0, 1))
-        word_table.append(late.tile([P, T], I32, name="word_table1", offset=0, align_bytes=64))
-        load_words(1, word_table[1])
+        w_raw.append(late.tile([P, PACK, M], F32, name="w_raw1", offset=0, align_bytes=64))
+        load_w(1, w_raw[1])
         place_scales((2, 3))
 
         gT_rows = gT.rearrange("(p t) c -> t p c", t=N_TILES)
         out_rows = out.rearrange("(p t) j -> p (t j)", t=N_TILES)
         gate_table = []
-        for t, slot in enumerate((1, 4, 2, 3)):
-            gates = late.tile([P, T], F32, name="gate_table%d" % t, offset=slot * WINDOW, align_bytes=64)
+        for t in range(N_TILES):
+            gates = late.tile([P, T], F32, name="gate_table%d" % t, offset=(2 * t + 1) * WINDOW // 2, align_bytes=64)
             nc.sync.dma_start(out=gates[:], in_=gT_rows[t])
             gate_table.append(gates)
 
-        w_codes, w_scales = [], []
-        for a in range(PASSES):
-            grouped = held.tile([P, M * PACK], BF16, name="w_grouped%d" % a, align_bytes=64)
-            nc.scalar.copy(
-                out=grouped[:].rearrange("p (t m i) -> p m t i", t=N_TILES, i=PACK),
-                in_=w_raw[a][:].rearrange("p i (m t) -> p m t i", t=N_TILES),
-            )
-            codes = held.tile([P, M], U32, name="w_codes%d" % a, align_bytes=64)
-            scales = held.tile([P, M], U8, name="w_scales%d" % a, align_bytes=64)
-            nc.vector.quantize_mx(out=codes[:].bitcast(FP8X4), scales=scales[:], in_=grouped[:])
-            w_codes.append(codes)
-            w_scales.append(scales)
+        w_mx = [[], []]
 
-        v_words = [[first_words[:, 0:HALF], first_words[:, HALF:S]], []]
-        for h in range(S // HALF):
-            picked = held.tile([P, HALF], U32, name="second_words%d" % h, align_bytes=64)
-            nc.vector.tensor_copy(
-                picked[:], word_table[1][:].bitcast(U32).indirect(entries(h * HALF, (h + 1) * HALF))
+        def quantise_w(a, t0, t1):
+            width = (t1 - t0) * P
+            grouped = held.tile([P, width * PACK], BF16, name="w_grouped%d_%d" % (a, t0), align_bytes=64)
+            nc.scalar.copy(
+                out=grouped[:].rearrange("p (t m i) -> p m t i", m=P, i=PACK),
+                in_=w_raw[a][:].rearrange("p i (m t) -> p m t i", t=N_TILES)[:, :, t0:t1, :],
             )
-            v_words[1].append(picked[:])
+            codes = held.tile([P, width], U32, name="w_codes%d_%d" % (a, t0), align_bytes=64)
+            scales = held.tile([P, width], U8, name="w_scales%d_%d" % (a, t0), align_bytes=64)
+            nc.vector.quantize_mx(out=codes[:].bitcast(FP8X4), scales=scales[:], in_=grouped[:])
+            for c0 in range(0, width, P):
+                w_mx[a].append((codes[:, c0 : c0 + P], scales[:, c0 : c0 + P]))
+
+        quantise_w(0, 0, N_TILES)
+        second_words = held.tile([P, S], U32, name="second_words", align_bytes=64)
+        nc.vector.tensor_copy(second_words[:], word_table[1][:].bitcast(U32).indirect(offsets[:]))
+        v_words = [first_words, second_words]
+        quantise_w(1, 0, N_TILES // 2)
+        quantise_w(1, N_TILES // 2, N_TILES)
 
         result = held.tile([P, N_TILES * S], F32, name="result")
         store_ends = [2 * S, 3 * S, 3 * S + LAST_CUT, 4 * S]
         stored = 0
         for t in range(N_TILES):
-            t_cols = slice(t * P, (t + 1) * P)
             biased = held.tile([P, S], F32, name="biased%d" % t)
-            for j0 in range(0, S, BANK):
-                h, c0 = divmod(j0, HALF)
-                acc = psum.tile([P, BANK], F32, name="acc")
-                for a in range(PASSES):
+            acc = [psum.tile([P, BANK], F32, name="acc") for j0 in range(0, S, BANK)]
+            for a in range(PASSES):
+                for bank, j0 in enumerate(range(0, S, BANK)):
                     nc.tensor.matmul_mx(
-                        out=acc[:],
-                        lhsT=w_codes[a][:, t_cols].bitcast(FP8X4),
-                        lhsT_scale=w_scales[a][:, t_cols],
-                        rhs=v_words[a][h][:, c0 : c0 + BANK].bitcast(FP8X4),
+                        out=acc[bank][:],
+                        lhsT=w_mx[a][t][0].bitcast(FP8X4),
+                        lhsT_scale=w_mx[a][t][1],
+                        rhs=v_words[a][:, j0 : j0 + BANK].bitcast(FP8X4),
                         rhs_scale=v_scales[SCALE_ROWS * a : P, j0 : j0 + BANK],
                         start=(a == 0),
                         stop=(a == PASSES - 1),
                     )
+            for bank, j0 in enumerate(range(0, S, BANK)):
                 nc.scalar.activation(
-                    out=biased[:, j0 : j0 + BANK], in_=acc[:], func=IDENTITY, bias=bias[:, t : t + 1]
+                    out=biased[:, j0 : j0 + BANK], in_=acc[bank][:], func=IDENTITY, bias=bias[:, t : t + 1]
                 )
 
             if t == 0:

@@ -1,6 +1,7 @@
 from contextlib import ExitStack
 
 import concourse.mybir as mybir
+from concourse.masks import make_identity
 
 K, M, T, S = 1024, 512, 4096, 2048
 FLOPS = 2 * K * M * S
@@ -36,6 +37,7 @@ def tile_list_tabgate_bias_kernel(tc, tab_words, tab_scales, w, gT, b, offs, out
         held = ctx.enter_context(tc.tile_pool(name="held", bufs=1))
         late = ctx.enter_context(tc.tile_pool(name="late", bufs=1))
         psum = ctx.enter_context(tc.psum_pool(name="psum", bufs=BANKS))
+        turn = ctx.enter_context(tc.psum_pool(name="turn", bufs=1))
 
         offsets = held.tile([P, S // LIST_ROWS], U16, name="offsets")
         nc.sync.dma_start(offsets[:], offs)
@@ -43,8 +45,6 @@ def tile_list_tabgate_bias_kernel(tc, tab_words, tab_scales, w, gT, b, offs, out
         def entries(j0, j1):
             return offsets[:, j0 // LIST_ROWS : j1 // LIST_ROWS]
 
-        bias = held.tile([P, N_TILES], F32, name="bias")
-        nc.sync.dma_start(out=bias[:], in_=b.rearrange("(p t) -> p t", t=N_TILES))
 
         scale_table = late.tile([P, T], U8, name="scale_table", offset=WINDOW // 2 - T // 2, align_bytes=64)
         nc.sync.dma_start(
@@ -54,6 +54,17 @@ def tile_list_tabgate_bias_kernel(tc, tab_words, tab_scales, w, gT, b, offs, out
         nc.vector.memset(scale_table[2 * QUADRANT : P, :].bitcast(I32), 0)
         v_scales = held.tile([P, S], U8, name="v_scales", align_bytes=64)
         nc.vector.memset(v_scales[:].bitcast(I32), 0)
+
+        bias_row = held.tile([P, M], F32, name="bias_row")
+        nc.vector.memset(bias_row[:], 0.0)
+        nc.sync.dma_start(out=bias_row[0:1, :], in_=b.rearrange("(o n) -> o n", o=1))
+        identity = held.tile([P, P], F32, name="identity")
+        make_identity(nc, identity[:])
+        turned = turn.tile([P, N_TILES, P], F32, name="turned")
+        for t in range(N_TILES):
+            nc.tensor.transpose(turned[:, t, :], bias_row[:, t:M:N_TILES], identity[:])
+        bias = held.tile([P, N_TILES], F32, name="bias")
+        nc.scalar.copy(out=bias[:], in_=turned[:, :, 0])
 
         def load_words(a, words):
             nc.sync.dma_start(out=words[:], in_=tab_words[a].rearrange("p c i -> p (c i)").bitcast(I32))
@@ -113,33 +124,40 @@ def tile_list_tabgate_bias_kernel(tc, tab_words, tab_scales, w, gT, b, offs, out
                 w_mx[a].append((codes[:, c0 : c0 + P], scales[:, c0 : c0 + P]))
 
         quantise_w(0, 0, N_TILES)
-        second_words = held.tile([P, S], U32, name="second_words", align_bytes=64)
-        nc.vector.tensor_copy(second_words[:], word_table[1][:].bitcast(U32).indirect(offsets[:]))
-        v_words = [first_words, second_words]
+        second_window = word_table[1][:].bitcast(U32)
+        second_words = held.tile([P, S - BANK], U32, name="second_words", align_bytes=64)
+        nc.vector.tensor_copy(second_words[:], second_window.indirect(entries(0, S - BANK)))
         quantise_w(1, 0, N_TILES // 2)
+        last_words = held.tile([P, BANK], U32, name="w_grouped1_0", align_bytes=64)
+        nc.vector.tensor_copy(last_words[:], second_window.indirect(entries(S - BANK, S)))
         quantise_w(1, N_TILES // 2, N_TILES)
+        v_words = [
+            [first_words[:, j0 : j0 + BANK] for j0 in range(0, S, BANK)],
+            [second_words[:, j0 : j0 + BANK] for j0 in range(0, S - BANK, BANK)] + [last_words[:]],
+        ]
 
         result = held.tile([P, N_TILES * S], F32, name="result")
         store_ends = [2 * S, 3 * S, 3 * S + LAST_CUT, 4 * S]
         stored = 0
         for t in range(N_TILES):
             biased = held.tile([P, S], F32, name="biased%d" % t)
-            acc = [psum.tile([P, BANK], F32, name="acc") for j0 in range(0, S, BANK)]
-            for a in range(PASSES):
-                for bank, j0 in enumerate(range(0, S, BANK)):
-                    nc.tensor.matmul_mx(
-                        out=acc[bank][:],
-                        lhsT=w_mx[a][t][0].bitcast(FP8X4),
-                        lhsT_scale=w_mx[a][t][1],
-                        rhs=v_words[a][:, j0 : j0 + BANK].bitcast(FP8X4),
-                        rhs_scale=v_scales[SCALE_ROWS * a : P, j0 : j0 + BANK],
-                        start=(a == 0),
-                        stop=(a == PASSES - 1),
+            for h0 in range(0, S, HALF):
+                acc = {j0: psum.tile([P, BANK], F32, name="acc") for j0 in range(h0, h0 + HALF, BANK)}
+                for a in range(PASSES):
+                    for j0 in acc:
+                        nc.tensor.matmul_mx(
+                            out=acc[j0][:],
+                            lhsT=w_mx[a][t][0].bitcast(FP8X4),
+                            lhsT_scale=w_mx[a][t][1],
+                            rhs=v_words[a][j0 // BANK].bitcast(FP8X4),
+                            rhs_scale=v_scales[SCALE_ROWS * a : P, j0 : j0 + BANK],
+                            start=(a == 0),
+                            stop=(a == PASSES - 1),
+                        )
+                for j0 in acc:
+                    nc.scalar.activation(
+                        out=biased[:, j0 : j0 + BANK], in_=acc[j0][:], func=IDENTITY, bias=bias[:, t : t + 1]
                     )
-            for bank, j0 in enumerate(range(0, S, BANK)):
-                nc.scalar.activation(
-                    out=biased[:, j0 : j0 + BANK], in_=acc[bank][:], func=IDENTITY, bias=bias[:, t : t + 1]
-                )
 
             if t == 0:
                 cuts = [0, HALF, S]

@@ -28,7 +28,7 @@ QUADRANT = 32
 SCALE_ROWS = 4
 BANKS = 4
 WINDOW = 4 * T
-LAST_CUT = 1408
+LAST_CUTS = [1216, 1792]
 
 
 def tile_list_tabgate_bias_kernel(tc, tab_words, tab_scales, w, gT, b, offs, out):
@@ -137,7 +137,7 @@ def tile_list_tabgate_bias_kernel(tc, tab_words, tab_scales, w, gT, b, offs, out
         ]
 
         result = held.tile([P, N_TILES * S], F32, name="result")
-        store_ends = [2 * S, 3 * S, 3 * S + LAST_CUT, 4 * S]
+        store_ends = [2 * S, 3 * S] + [3 * S + cut for cut in LAST_CUTS] + [4 * S]
         stored = 0
         for t in range(N_TILES):
             biased = held.tile([P, S], F32, name="biased%d" % t)
@@ -162,7 +162,7 @@ def tile_list_tabgate_bias_kernel(tc, tab_words, tab_scales, w, gT, b, offs, out
             if t == 0:
                 cuts = [0, HALF, S]
             elif t == N_TILES - 1:
-                cuts = [0, LAST_CUT, S]
+                cuts = [0] + LAST_CUTS + [S]
             else:
                 cuts = [0, S]
             for j0, j1 in zip(cuts, cuts[1:]):

@@ -26,6 +26,7 @@ HALF = S // 2
 LIST_ROWS = 16
 QUADRANT = 32
 SCALE_ROWS = 4
+STAGED = 48
 BANKS = 4
 WINDOW = 4 * T
 LAST_CUTS = [1216, 1792]
@@ -47,11 +48,11 @@ def tile_list_tabgate_bias_kernel(tc, tab_words, tab_scales, w, gT, b, offs, out
 
 
         scale_table = late.tile([P, T], U8, name="scale_table", offset=WINDOW // 2 - T // 2, align_bytes=64)
-        nc.sync.dma_start(
-            out=scale_table[0:QUADRANT, :].bitcast(I32), in_=tab_scales.rearrange("a q c -> (a q) c").bitcast(I32)
-        )
-        nc.vector.memset(scale_table[QUADRANT : 2 * QUADRANT, :].bitcast(I32), 0)
-        nc.vector.memset(scale_table[2 * QUADRANT : P, :].bitcast(I32), 0)
+        for a in range(PASSES):
+            nc.sync.dma_start(
+                out=scale_table[64 * a + STAGED : 64 * (a + 1), :].bitcast(I32), in_=tab_scales[a].bitcast(I32)
+            )
+            nc.vector.memset(scale_table[64 * a : 64 * a + STAGED, :].bitcast(I32), 0)
         v_scales = held.tile([P, S], U8, name="v_scales", align_bytes=64)
         nc.vector.memset(v_scales[:].bitcast(I32), 0)
 
@@ -92,7 +93,7 @@ def tile_list_tabgate_bias_kernel(tc, tab_words, tab_scales, w, gT, b, offs, out
                 for a in range(PASSES):
                     nc.sync.dma_start(
                         out=v_scales[SCALE_ROWS * a + r : P : QUADRANT, :].bitcast(I32),
-                        in_=picked_scales[16 * a + r : 16 * (a + 1) : SCALE_ROWS, :].bitcast(I32),
+                        in_=picked_scales[64 * a + STAGED + r : 64 * (a + 1) : SCALE_ROWS, :].bitcast(I32),
                     )
 
         place_scales((0, 1))

@@ -21,12 +21,13 @@ PACK = 4
 K_PASS = P * PACK
 PASSES = K // K_PASS
 N_TILES = M // P
+PAIR = 2
 BANK = 512
 HALF = S // 2
 LIST_ROWS = 16
 QUADRANT = 32
 SCALE_ROWS = 4
-STAGED = 48
+STAGED = P - QUADRANT
 BANKS = 4
 WINDOW = 4 * T
 LAST_CUTS = [1216, 1792]
@@ -48,11 +49,10 @@ def tile_list_tabgate_bias_kernel(tc, tab_words, tab_scales, w, gT, b, offs, out
 
 
         scale_table = late.tile([P, T], U8, name="scale_table", offset=WINDOW // 2 - T // 2, align_bytes=64)
-        for a in range(PASSES):
-            nc.sync.dma_start(
-                out=scale_table[64 * a + STAGED : 64 * (a + 1), :].bitcast(I32), in_=tab_scales[a].bitcast(I32)
-            )
-            nc.vector.memset(scale_table[64 * a : 64 * a + STAGED, :].bitcast(I32), 0)
+        nc.sync.dma_start(
+            out=scale_table[STAGED:P, :].bitcast(I32), in_=tab_scales.rearrange("a q c -> (a q) c").bitcast(I32)
+        )
+        nc.vector.memset(scale_table[0:STAGED, :].bitcast(I32), 0)
         v_scales = held.tile([P, S], U8, name="v_scales", align_bytes=64)
         nc.vector.memset(v_scales[:].bitcast(I32), 0)
 
@@ -63,7 +63,8 @@ def tile_list_tabgate_bias_kernel(tc, tab_words, tab_scales, w, gT, b, offs, out
         make_identity(nc, identity[:])
         turned = turn.tile([P, N_TILES, P], F32, name="turned")
         for t in range(N_TILES):
-            nc.tensor.transpose(turned[:, t, :], bias_row[:, t:M:N_TILES], identity[:])
+            h, u = divmod(t, PAIR)
+            nc.tensor.transpose(turned[:, t, :], bias_row[:, h * PAIR * P + u : (h + 1) * PAIR * P : PAIR], identity[:])
         bias = held.tile([P, N_TILES], F32, name="bias")
         nc.scalar.copy(out=bias[:], in_=turned[:, :, 0])
 
@@ -93,7 +94,7 @@ def tile_list_tabgate_bias_kernel(tc, tab_words, tab_scales, w, gT, b, offs, out
                 for a in range(PASSES):
                     nc.sync.dma_start(
                         out=v_scales[SCALE_ROWS * a + r : P : QUADRANT, :].bitcast(I32),
-                        in_=picked_scales[64 * a + STAGED + r : 64 * (a + 1) : SCALE_ROWS, :].bitcast(I32),
+                        in_=picked_scales[STAGED + 16 * a + r : STAGED + 16 * (a + 1) : SCALE_ROWS, :].bitcast(I32),
                     )
 
         place_scales((0, 1))
@@ -101,22 +102,22 @@ def tile_list_tabgate_bias_kernel(tc, tab_words, tab_scales, w, gT, b, offs, out
         load_w(1, w_raw[1])
         place_scales((2, 3))
 
-        gT_rows = gT.rearrange("(p t) c -> t p c", t=N_TILES)
-        out_rows = out.rearrange("(p t) j -> p (t j)", t=N_TILES)
+        gT_rows = gT.rearrange("(h p u) c -> h u p c", p=P, u=PAIR)
+        out_rows = out.rearrange("(h p u) j -> h p (u j)", p=P, u=PAIR)
         gate_table = []
         for t in range(N_TILES):
             gates = late.tile([P, T], F32, name="gate_table%d" % t, offset=(2 * t + 1) * WINDOW // 2, align_bytes=64)
-            nc.sync.dma_start(out=gates[:], in_=gT_rows[t])
+            nc.sync.dma_start(out=gates[:], in_=gT_rows[t // PAIR, t % PAIR])
             gate_table.append(gates)
 
         w_mx = [[], []]
 
-        def quantise_w(a, t0, t1):
+        def quantise_w(a, t0, t1, copy):
             width = (t1 - t0) * P
             grouped = held.tile([P, width * PACK], BF16, name="w_grouped%d_%d" % (a, t0), align_bytes=64)
-            nc.scalar.copy(
-                out=grouped[:].rearrange("p (t m i) -> p m t i", m=P, i=PACK),
-                in_=w_raw[a][:].rearrange("p i (m t) -> p m t i", t=N_TILES)[:, :, t0:t1, :],
+            copy(
+                out=grouped[:].rearrange("p (h u m i) -> p h m u i", u=PAIR, m=P, i=PACK),
+                in_=w_raw[a][:, :, t0 * P : t1 * P].rearrange("p i (h m u) -> p h m u i", m=P, u=PAIR),
             )
             codes = held.tile([P, width], U32, name="w_codes%d_%d" % (a, t0), align_bytes=64)
             scales = held.tile([P, width], U8, name="w_scales%d_%d" % (a, t0), align_bytes=64)
@@ -124,17 +125,17 @@ def tile_list_tabgate_bias_kernel(tc, tab_words, tab_scales, w, gT, b, offs, out
             for c0 in range(0, width, P):
                 w_mx[a].append((codes[:, c0 : c0 + P], scales[:, c0 : c0 + P]))
 
-        quantise_w(0, 0, N_TILES)
+        quantise_w(0, 0, N_TILES, nc.scalar.copy)
         second_window = word_table[1][:].bitcast(U32)
-        second_words = held.tile([P, S - BANK], U32, name="second_words", align_bytes=64)
-        nc.vector.tensor_copy(second_words[:], second_window.indirect(entries(0, S - BANK)))
-        quantise_w(1, 0, N_TILES // 2)
-        last_words = held.tile([P, BANK], U32, name="w_grouped1_0", align_bytes=64)
-        nc.vector.tensor_copy(last_words[:], second_window.indirect(entries(S - BANK, S)))
-        quantise_w(1, N_TILES // 2, N_TILES)
+        second_words = held.tile([P, HALF], U32, name="second_words", align_bytes=64)
+        nc.vector.tensor_copy(second_words[:], second_window.indirect(entries(0, HALF)))
+        quantise_w(1, 0, PAIR, nc.vector.tensor_copy)
+        last_words = held.tile([P, HALF], U32, name="w_grouped1_0", align_bytes=64)
+        nc.vector.tensor_copy(last_words[:], second_window.indirect(entries(HALF, S)))
+        quantise_w(1, PAIR, N_TILES, nc.scalar.copy)
         v_words = [
             [first_words[:, j0 : j0 + BANK] for j0 in range(0, S, BANK)],
-            [second_words[:, j0 : j0 + BANK] for j0 in range(0, S - BANK, BANK)] + [last_words[:]],
+            [words[:, j0 : j0 + BANK] for words in (second_words, last_words) for j0 in range(0, HALF, BANK)],
         ]
 
         result = held.tile([P, N_TILES * S], F32, name="result")
@@ -175,6 +176,6 @@ def tile_list_tabgate_bias_kernel(tc, tab_words, tab_scales, w, gT, b, offs, out
                     MULT,
                 )
                 if done in store_ends:
-                    cols = slice(stored, done)
-                    nc.sync.dma_start(out=out_rows[:, cols], in_=result[:, cols])
+                    base = t // PAIR * PAIR * S
+                    nc.sync.dma_start(out=out_rows[t // PAIR][:, stored - base : done - base], in_=result[:, stored:done])
                     stored = done

@@ -112,10 +112,10 @@ def tile_list_tabgate_bias_kernel(tc, tab_words, tab_scales, w, gT, b, offs, out
 
         w_mx = [[], []]
 
-        def quantise_w(a, t0, t1, copy):
+        def quantise_w(a, t0, t1):
             width = (t1 - t0) * P
             grouped = held.tile([P, width * PACK], BF16, name="w_grouped%d_%d" % (a, t0), align_bytes=64)
-            copy(
+            nc.scalar.copy(
                 out=grouped[:].rearrange("p (h u m i) -> p h m u i", u=PAIR, m=P, i=PACK),
                 in_=w_raw[a][:, :, t0 * P : t1 * P].rearrange("p i (h m u) -> p h m u i", m=P, u=PAIR),
             )
@@ -125,17 +125,17 @@ def tile_list_tabgate_bias_kernel(tc, tab_words, tab_scales, w, gT, b, offs, out
             for c0 in range(0, width, P):
                 w_mx[a].append((codes[:, c0 : c0 + P], scales[:, c0 : c0 + P]))
 
-        quantise_w(0, 0, N_TILES, nc.scalar.copy)
+        quantise_w(0, 0, N_TILES)
         second_window = word_table[1][:].bitcast(U32)
-        second_words = held.tile([P, HALF], U32, name="second_words", align_bytes=64)
-        nc.vector.tensor_copy(second_words[:], second_window.indirect(entries(0, HALF)))
-        quantise_w(1, 0, PAIR, nc.vector.tensor_copy)
-        last_words = held.tile([P, HALF], U32, name="w_grouped1_0", align_bytes=64)
-        nc.vector.tensor_copy(last_words[:], second_window.indirect(entries(HALF, S)))
-        quantise_w(1, PAIR, N_TILES, nc.scalar.copy)
+        second_words = held.tile([P, S - BANK], U32, name="second_words", align_bytes=64)
+        nc.vector.tensor_copy(second_words[:], second_window.indirect(entries(0, S - BANK)))
+        quantise_w(1, 0, PAIR)
+        last_words = held.tile([P, BANK], U32, name="w_grouped1_0", align_bytes=64)
+        nc.vector.tensor_copy(last_words[:], second_window.indirect(entries(S - BANK, S)))
+        quantise_w(1, PAIR, N_TILES)
         v_words = [
             [first_words[:, j0 : j0 + BANK] for j0 in range(0, S, BANK)],
-            [words[:, j0 : j0 + BANK] for words in (second_words, last_words) for j0 in range(0, HALF, BANK)],
+            [second_words[:, j0 : j0 + BANK] for j0 in range(0, S - BANK, BANK)] + [last_words[:]],
         ]
 
         result = held.tile([P, N_TILES * S], F32, name="result")

@@ -30,7 +30,7 @@ SCALE_ROWS = 4
 STAGED = P - QUADRANT
 BANKS = 4
 WINDOW = 4 * T
-LAST_CUTS = [1216, 1792]
+LAST_CUTS = [1120, 1664, 1920]
 
 
 def tile_list_tabgate_bias_kernel(tc, tab_words, tab_scales, w, gT, b, offs, out):
@@ -58,7 +58,7 @@ def tile_list_tabgate_bias_kernel(tc, tab_words, tab_scales, w, gT, b, offs, out
 
         bias_row = held.tile([P, M], F32, name="bias_row")
         nc.vector.memset(bias_row[:], 0.0)
-        nc.sync.dma_start(out=bias_row[0:1, :], in_=b.rearrange("(o n) -> o n", o=1))
+        nc.gpsimd.dma_start(out=bias_row[0:1, :], in_=b.rearrange("(o n) -> o n", o=1))
         identity = held.tile([P, P], F32, name="identity")
         make_identity(nc, identity[:])
         turned = turn.tile([P, N_TILES, P], F32, name="turned")

@@ -28,7 +28,7 @@ LIST_ROWS = 16
 QUADRANT = 32
 SCALE_ROWS = 4
 STAGED = P - QUADRANT
-BANKS = 4
+BANKS = 3
 WINDOW = 4 * T
 LAST_CUTS = [1120, 1664, 1920]
 
@@ -115,10 +115,21 @@ def tile_list_tabgate_bias_kernel(tc, tab_words, tab_scales, w, gT, b, offs, out
         def quantise_w(a, t0, t1):
             width = (t1 - t0) * P
             grouped = held.tile([P, width * PACK], BF16, name="w_grouped%d_%d" % (a, t0), align_bytes=64)
-            nc.scalar.copy(
-                out=grouped[:].rearrange("p (h u m i) -> p h m u i", u=PAIR, m=P, i=PACK),
-                in_=w_raw[a][:, :, t0 * P : t1 * P].rearrange("p i (h m u) -> p h m u i", m=P, u=PAIR),
-            )
+            by_feature = w_raw[a][:].rearrange("p i (h m u) -> p h m u i", m=P, u=PAIR)
+            t = t0
+            while t < t1:
+                h, u = divmod(t, PAIR)
+                halves = (t1 - t) // PAIR if u == 0 else 0
+                count = halves * PAIR if halves else 1
+                part = grouped[:, (t - t0) * P * PACK : (t - t0 + count) * P * PACK]
+                if halves:
+                    nc.scalar.copy(
+                        out=part.rearrange("p (h u m i) -> p h m u i", u=PAIR, m=P, i=PACK),
+                        in_=by_feature[:, h : h + halves],
+                    )
+                else:
+                    nc.scalar.copy(out=part.rearrange("p (m i) -> p m i", i=PACK), in_=by_feature[:, h, :, u, :])
+                t = t + count
             codes = held.tile([P, width], U32, name="w_codes%d_%d" % (a, t0), align_bytes=64)
             scales = held.tile([P, width], U8, name="w_scales%d_%d" % (a, t0), align_bytes=64)
             nc.vector.quantize_mx(out=codes[:].bitcast(FP8X4), scales=scales[:], in_=grouped[:])
@@ -129,10 +140,10 @@ def tile_list_tabgate_bias_kernel(tc, tab_words, tab_scales, w, gT, b, offs, out
         second_window = word_table[1][:].bitcast(U32)
         second_words = held.tile([P, S - BANK], U32, name="second_words", align_bytes=64)
         nc.vector.tensor_copy(second_words[:], second_window.indirect(entries(0, S - BANK)))
-        quantise_w(1, 0, PAIR)
+        quantise_w(1, 0, 1)
         last_words = held.tile([P, BANK], U32, name="w_grouped1_0", align_bytes=64)
         nc.vector.tensor_copy(last_words[:], second_window.indirect(entries(S - BANK, S)))
-        quantise_w(1, PAIR, N_TILES)
+        quantise_w(1, 1, N_TILES)
         v_words = [
             [first_words[:, j0 : j0 + BANK] for j0 in range(0, S, BANK)],
             [second_words[:, j0 : j0 + BANK] for j0 in range(0, S - BANK, BANK)] + [last_words[:]],
@@ -162,7 +173,7 @@ def tile_list_tabgate_bias_kernel(tc, tab_words, tab_scales, w, gT, b, offs, out
                     )
 
             if t == 0:
-                cuts = [0, HALF, S]
+                cuts = [0, BANK, S]
             elif t == N_TILES - 1:
                 cuts = [0] + LAST_CUTS + [S]
             else:

@@ -27,7 +27,8 @@ HALF = S // 2
 LIST_ROWS = 16
 QUADRANT = 32
 SCALE_ROWS = 4
-STAGED = P - QUADRANT
+BLOCK = 8
+HEAD = 768
 BANKS = 3
 WINDOW = 4 * T
 LAST_CUTS = [1120, 1664, 1920]
@@ -47,32 +48,27 @@ def tile_list_tabgate_bias_kernel(tc, tab_words, tab_scales, w, gT, b, offs, out
         def entries(j0, j1):
             return offsets[:, j0 // LIST_ROWS : j1 // LIST_ROWS]
 
+        def load_words(a, words, c0, c1):
+            nc.sync.dma_start(out=words[:, c0:c1], in_=tab_words[a].rearrange("p c i -> p (c i)").bitcast(I32)[:, c0:c1])
 
         scale_table = late.tile([P, T], U8, name="scale_table", offset=WINDOW // 2 - T // 2, align_bytes=64)
-        nc.sync.dma_start(
-            out=scale_table[STAGED:P, :].bitcast(I32), in_=tab_scales.rearrange("a q c -> (a q) c").bitcast(I32)
-        )
-        nc.vector.memset(scale_table[0:STAGED, :].bitcast(I32), 0)
-        v_scales = held.tile([P, S], U8, name="v_scales", align_bytes=64)
-        nc.vector.memset(v_scales[:].bitcast(I32), 0)
+        nc.vector.memset(scale_table[:].bitcast(I32), 0)
+        word_table = [late.tile([P, T], I32, name="word_table0", offset=2 * WINDOW, align_bytes=64)]
+        load_words(0, word_table[0], 0, HEAD)
+        for a in range(PASSES):
+            nc.sync.dma_start(out=scale_table[SCALE_ROWS * a : P : BLOCK, :].bitcast(I32), in_=tab_scales[a].bitcast(I32))
+        load_words(0, word_table[0], HEAD, T)
 
         bias_row = held.tile([P, M], F32, name="bias_row")
         nc.vector.memset(bias_row[:], 0.0)
         nc.gpsimd.dma_start(out=bias_row[0:1, :], in_=b.rearrange("(o n) -> o n", o=1))
         identity = held.tile([P, P], F32, name="identity")
-        make_identity(nc, identity[:])
+        nc.vector.memset(identity[:], 0.0)
+        make_identity(nc, identity[:], nomemset=True)
         turned = turn.tile([P, N_TILES, P], F32, name="turned")
         for t in range(N_TILES):
             h, u = divmod(t, PAIR)
             nc.tensor.transpose(turned[:, t, :], bias_row[:, h * PAIR * P + u : (h + 1) * PAIR * P : PAIR], identity[:])
-        bias = held.tile([P, N_TILES], F32, name="bias")
-        nc.scalar.copy(out=bias[:], in_=turned[:, :, 0])
-
-        def load_words(a, words):
-            nc.sync.dma_start(out=words[:], in_=tab_words[a].rearrange("p c i -> p (c i)").bitcast(I32))
-
-        word_table = [late.tile([P, T], I32, name="word_table0", offset=2 * WINDOW, align_bytes=64)]
-        load_words(0, word_table[0])
 
         def load_w(a, raw):
             nc.sync.dma_start(
@@ -82,25 +78,31 @@ def tile_list_tabgate_bias_kernel(tc, tab_words, tab_scales, w, gT, b, offs, out
         w_raw = [held.tile([P, PACK, M], F32, name="w_raw0")]
         load_w(0, w_raw[0])
         word_table.append(held.tile([P, T], I32, name="word_table1", align_bytes=64))
-        load_words(1, word_table[1])
+        load_words(1, word_table[1], 0, T)
 
         picked_scales = late.tile([P, S], U8, name="picked_scales", offset=9 * WINDOW // 2 - S, align_bytes=64)
-        nc.vector.tensor_copy(picked_scales[:], scale_table[:].indirect(offsets[:]))
+        parts = [(0, S - BANK), (S - BANK, S)]
+        for j0, j1 in parts:
+            nc.vector.tensor_copy(picked_scales[:, j0:j1], scale_table[:].indirect(entries(j0, j1)))
+        v_scales = held.tile([P, S], U8, name="v_scales", align_bytes=64)
+        for j0, j1 in parts:
+            nc.vector.tensor_copy(v_scales[:, j0:j1].bitcast(I32), picked_scales[:, j0:j1].bitcast(I32))
         first_words = held.tile([P, S], U32, name="first_words", align_bytes=64)
         nc.vector.tensor_copy(first_words[:], word_table[0][:].bitcast(U32).indirect(offsets[:]))
 
-        def place_scales(rows):
-            for r in rows:
-                for a in range(PASSES):
-                    nc.sync.dma_start(
-                        out=v_scales[SCALE_ROWS * a + r : P : QUADRANT, :].bitcast(I32),
-                        in_=picked_scales[STAGED + 16 * a + r : STAGED + 16 * (a + 1) : SCALE_ROWS, :].bitcast(I32),
-                    )
+        moves = [(r, a) for r in range(1, SCALE_ROWS) for a in range(PASSES)]
 
-        place_scales((0, 1))
+        def place_scales(some):
+            for r, a in some:
+                nc.sync.dma_start(
+                    out=v_scales[SCALE_ROWS * a + r : P : QUADRANT, :].bitcast(I32),
+                    in_=picked_scales[SCALE_ROWS * a + BLOCK * r : P : QUADRANT, :].bitcast(I32),
+                )
+
+        place_scales(moves[:3])
         w_raw.append(late.tile([P, PACK, M], F32, name="w_raw1", offset=0, align_bytes=64))
         load_w(1, w_raw[1])
-        place_scales((2, 3))
+        place_scales(moves[3:])
 
         gT_rows = gT.rearrange("(h p u) c -> h u p c", p=P, u=PAIR)
         out_rows = out.rearrange("(h p u) j -> h p (u j)", p=P, u=PAIR)
@@ -137,6 +139,8 @@ def tile_list_tabgate_bias_kernel(tc, tab_words, tab_scales, w, gT, b, offs, out
                 w_mx[a].append((codes[:, c0 : c0 + P], scales[:, c0 : c0 + P]))
 
         quantise_w(0, 0, N_TILES)
+        bias = held.tile([P, N_TILES], F32, name="w_raw0")
+        nc.scalar.copy(out=bias[:], in_=turned[:, :, 0])
         second_window = word_table[1][:].bitcast(U32)
         second_words = held.tile([P, S - BANK], U32, name="second_words", align_bytes=64)
         nc.vector.tensor_copy(second_words[:], second_window.indirect(entries(0, S - BANK)))

@@ -39,7 +39,7 @@ def tile_list_tabgate_bias_kernel(tc, tab_words, tab_scales, w, gT, b, offs, out
     with ExitStack() as ctx:
         held = ctx.enter_context(tc.tile_pool(name="held", bufs=1))
         late = ctx.enter_context(tc.tile_pool(name="late", bufs=1))
-        psum = ctx.enter_context(tc.psum_pool(name="psum", bufs=BANKS))
+        psum = ctx.enter_context(tc.psum_pool(name="psum", bufs=1))
         turn = ctx.enter_context(tc.psum_pool(name="turn", bufs=1))
 
         offsets = held.tile([P, S // LIST_ROWS], U16, name="offsets")
@@ -81,28 +81,28 @@ def tile_list_tabgate_bias_kernel(tc, tab_words, tab_scales, w, gT, b, offs, out
         load_words(1, word_table[1], 0, T)
 
         picked_scales = late.tile([P, S], U8, name="picked_scales", offset=9 * WINDOW // 2 - S, align_bytes=64)
-        parts = [(0, S - BANK), (S - BANK, S)]
+        parts = [(0, HALF), (HALF, S)]
         for j0, j1 in parts:
             nc.vector.tensor_copy(picked_scales[:, j0:j1], scale_table[:].indirect(entries(j0, j1)))
-        v_scales = held.tile([P, S], U8, name="v_scales", align_bytes=64)
-        for j0, j1 in parts:
-            nc.vector.tensor_copy(v_scales[:, j0:j1].bitcast(I32), picked_scales[:, j0:j1].bitcast(I32))
+        v_scales = [held.tile([P, HALF], U8, name="v_scales%d" % h, align_bytes=64) for h in range(2)]
+        for h, (j0, j1) in enumerate(parts):
+            nc.vector.tensor_copy(v_scales[h][:].bitcast(I32), picked_scales[:, j0:j1].bitcast(I32))
         first_words = held.tile([P, S], U32, name="first_words", align_bytes=64)
         nc.vector.tensor_copy(first_words[:], word_table[0][:].bitcast(U32).indirect(offsets[:]))
 
         moves = [(r, a) for r in range(1, SCALE_ROWS) for a in range(PASSES)]
 
-        def place_scales(some):
+        def place_scales(h, some):
             for r, a in some:
                 nc.sync.dma_start(
-                    out=v_scales[SCALE_ROWS * a + r : P : QUADRANT, :].bitcast(I32),
-                    in_=picked_scales[SCALE_ROWS * a + BLOCK * r : P : QUADRANT, :].bitcast(I32),
+                    out=v_scales[h][SCALE_ROWS * a + r : P : QUADRANT, :].bitcast(I32),
+                    in_=picked_scales[SCALE_ROWS * a + BLOCK * r : P : QUADRANT, h * HALF : (h + 1) * HALF].bitcast(I32),
                 )
 
-        place_scales(moves[:3])
+        place_scales(0, moves[:3])
         w_raw.append(late.tile([P, PACK, M], F32, name="w_raw1", offset=0, align_bytes=64))
         load_w(1, w_raw[1])
-        place_scales(moves[3:])
+        place_scales(0, moves[3:])
 
         gT_rows = gT.rearrange("(h p u) c -> h u p c", p=P, u=PAIR)
         out_rows = out.rearrange("(h p u) j -> h p (u j)", p=P, u=PAIR)
@@ -111,6 +111,8 @@ def tile_list_tabgate_bias_kernel(tc, tab_words, tab_scales, w, gT, b, offs, out
             gates = late.tile([P, T], F32, name="gate_table%d" % t, offset=(2 * t + 1) * WINDOW // 2, align_bytes=64)
             nc.sync.dma_start(out=gates[:], in_=gT_rows[t // PAIR, t % PAIR])
             gate_table.append(gates)
+            if t == 0:
+                place_scales(1, moves)
 
         w_mx = [[], []]
 
@@ -159,25 +161,26 @@ def tile_list_tabgate_bias_kernel(tc, tab_words, tab_scales, w, gT, b, offs, out
         for t in range(N_TILES):
             biased = held.tile([P, S], F32, name="biased%d" % t)
             for h0 in range(0, S, HALF):
-                acc = {j0: psum.tile([P, BANK], F32, name="acc") for j0 in range(h0, h0 + HALF, BANK)}
-                for a in range(PASSES):
-                    for j0 in acc:
-                        nc.tensor.matmul_mx(
-                            out=acc[j0][:],
-                            lhsT=w_mx[a][t][0].bitcast(FP8X4),
-                            lhsT_scale=w_mx[a][t][1],
-                            rhs=v_words[a][j0 // BANK].bitcast(FP8X4),
-                            rhs_scale=v_scales[SCALE_ROWS * a : P, j0 : j0 + BANK],
-                            start=(a == 0),
-                            stop=(a == PASSES - 1),
-                        )
+                acc = {j0: psum.tile([P, BANK], F32, name="acc%d" % ((t * S + j0) // BANK % BANKS)) for j0 in range(h0, h0 + HALF, BANK)}
+                by_bank = t == 0 and h0 > 0
+                steps = [(a, j0) for a in range(PASSES) for j0 in acc]
+                for a, j0 in sorted(steps, key=lambda s: s[1]) if by_bank else steps:
+                    nc.tensor.matmul_mx(
+                        out=acc[j0][:],
+                        lhsT=w_mx[a][t][0].bitcast(FP8X4),
+                        lhsT_scale=w_mx[a][t][1],
+                        rhs=v_words[a][j0 // BANK].bitcast(FP8X4),
+                        rhs_scale=v_scales[h0 // HALF][SCALE_ROWS * a : P, j0 - h0 : j0 - h0 + BANK],
+                        start=(a == 0),
+                        stop=(a == PASSES - 1),
+                    )
                 for j0 in acc:
                     nc.scalar.activation(
                         out=biased[:, j0 : j0 + BANK], in_=acc[j0][:], func=IDENTITY, bias=bias[:, t : t + 1]
                     )
 
             if t == 0:
-                cuts = [0, BANK, S]
+                cuts = list(range(0, S + 1, BANK))
             elif t == N_TILES - 1:
                 cuts = [0] + LAST_CUTS + [S]
             else:

@@ -158,29 +158,35 @@ def tile_list_tabgate_bias_kernel(tc, tab_words, tab_scales, w, gT, b, offs, out
         result = held.tile([P, N_TILES * S], F32, name="result")
         store_ends = [2 * S, 3 * S] + [3 * S + cut for cut in LAST_CUTS] + [4 * S]
         stored = 0
-        for t in range(N_TILES):
-            biased = held.tile([P, S], F32, name="biased%d" % t)
-            for h0 in range(0, S, HALF):
-                acc = {j0: psum.tile([P, BANK], F32, name="acc%d" % ((t * S + j0) // BANK % BANKS)) for j0 in range(h0, h0 + HALF, BANK)}
-                by_bank = t == 0 and h0 > 0
-                steps = [(a, j0) for a in range(PASSES) for j0 in acc]
-                for a, j0 in sorted(steps, key=lambda s: s[1]) if by_bank else steps:
-                    nc.tensor.matmul_mx(
-                        out=acc[j0][:],
-                        lhsT=w_mx[a][t][0].bitcast(FP8X4),
-                        lhsT_scale=w_mx[a][t][1],
-                        rhs=v_words[a][j0 // BANK].bitcast(FP8X4),
-                        rhs_scale=v_scales[h0 // HALF][SCALE_ROWS * a : P, j0 - h0 : j0 - h0 + BANK],
-                        start=(a == 0),
-                        stop=(a == PASSES - 1),
-                    )
-                for j0 in acc:
-                    nc.scalar.activation(
-                        out=biased[:, j0 : j0 + BANK], in_=acc[j0][:], func=IDENTITY, bias=bias[:, t : t + 1]
-                    )
+        biased = [held.tile([P, S], F32, name="biased%d" % t) for t in range(N_TILES)]
+        turns = [(t0 + u, h0) for t0 in range(0, N_TILES, PAIR) for h0 in range(0, S, HALF) for u in range(PAIR)]
+        for i, (t, h0) in enumerate(turns):
+            acc = {}
+            for k, j0 in enumerate(range(h0, h0 + HALF, BANK)):
+                acc[j0] = psum.tile([P, BANK], F32, name="acc%d" % ((HALF // BANK * i + k) % BANKS))
+            steps = [(a, j0) for a in range(PASSES) for j0 in acc]
+            if t == 0 and h0 > 0:
+                steps = [(a, j0) for j0 in acc for a in range(PASSES)]
+            for a, j0 in steps:
+                nc.tensor.matmul_mx(
+                    out=acc[j0][:],
+                    lhsT=w_mx[a][t][0].bitcast(FP8X4),
+                    lhsT_scale=w_mx[a][t][1],
+                    rhs=v_words[a][j0 // BANK].bitcast(FP8X4),
+                    rhs_scale=v_scales[h0 // HALF][SCALE_ROWS * a : P, j0 - h0 : j0 - h0 + BANK],
+                    start=(a == 0),
+                    stop=(a == PASSES - 1),
+                )
+            for j0 in acc:
+                nc.scalar.activation(
+                    out=biased[t][:, j0 : j0 + BANK], in_=acc[j0][:], func=IDENTITY, bias=bias[:, t : t + 1]
+                )
 
+        for t in range(N_TILES):
             if t == 0:
                 cuts = list(range(0, S + 1, BANK))
+            elif t == 1:
+                cuts = [0, HALF, S]
             elif t == N_TILES - 1:
                 cuts = [0] + LAST_CUTS + [S]
             else:
@@ -190,7 +196,7 @@ def tile_list_tabgate_bias_kernel(tc, tab_words, tab_scales, w, gT, b, offs, out
                 nc.vector.tensor_tensor(
                     result[:, t * S + j0 : done],
                     gate_table[t][:].indirect(entries(j0, j1)),
-                    biased[:, j0:j1],
+                    biased[t][:, j0:j1],
                     MULT,
                 )
                 if done in store_ends:

@@ -26,8 +26,7 @@ BANK = 512
 HALF = S // 2
 LIST_ROWS = 16
 QUADRANT = 32
-SCALE_ROWS = 4
-BLOCK = 8
+PASS_ROW = 8
 HEAD = 768
 BANKS = 3
 WINDOW = 4 * T
@@ -55,13 +54,14 @@ def tile_list_tabgate_bias_kernel(tc, tab_words, tab_scales, w, gT, b, offs, out
         nc.vector.memset(scale_table[:].bitcast(I32), 0)
         word_table = [late.tile([P, T], I32, name="word_table0", offset=2 * WINDOW, align_bytes=64)]
         load_words(0, word_table[0], 0, HEAD)
-        for a in range(PASSES):
-            nc.sync.dma_start(out=scale_table[SCALE_ROWS * a : P : BLOCK, :].bitcast(I32), in_=tab_scales[a].bitcast(I32))
+        by_parity = tab_scales.bitcast(I32).rearrange("a (u e) c -> e u a c", e=2)
+        for e in range(2):
+            nc.sync.dma_start(out=scale_table[e:P:PASS_ROW, :].bitcast(I32), in_=by_parity[e])
         load_words(0, word_table[0], HEAD, T)
 
         bias_row = held.tile([P, M], F32, name="bias_row")
         nc.vector.memset(bias_row[:], 0.0)
-        nc.gpsimd.dma_start(out=bias_row[0:1, :], in_=b.rearrange("(o n) -> o n", o=1))
+        nc.sync.dma_start(out=bias_row[0:1, :], in_=b.rearrange("(o n) -> o n", o=1))
         identity = held.tile([P, P], F32, name="identity")
         nc.vector.memset(identity[:], 0.0)
         make_identity(nc, identity[:], nomemset=True)
@@ -84,25 +84,23 @@ def tile_list_tabgate_bias_kernel(tc, tab_words, tab_scales, w, gT, b, offs, out
         parts = [(0, HALF), (HALF, S)]
         for j0, j1 in parts:
             nc.vector.tensor_copy(picked_scales[:, j0:j1], scale_table[:].indirect(entries(j0, j1)))
-        v_scales = [held.tile([P, HALF], U8, name="v_scales%d" % h, align_bytes=64) for h in range(2)]
-        for h, (j0, j1) in enumerate(parts):
-            nc.vector.tensor_copy(v_scales[h][:].bitcast(I32), picked_scales[:, j0:j1].bitcast(I32))
+        v_scales = held.tile([P, S], U8, name="v_scales", align_bytes=64)
+        for j0, j1 in parts:
+            nc.vector.tensor_copy(v_scales[:, j0:j1].bitcast(I32), picked_scales[:, j0:j1].bitcast(I32))
         first_words = held.tile([P, S], U32, name="first_words", align_bytes=64)
         nc.vector.tensor_copy(first_words[:], word_table[0][:].bitcast(U32).indirect(offsets[:]))
 
-        moves = [(r, a) for r in range(1, SCALE_ROWS) for a in range(PASSES)]
-
-        def place_scales(h, some):
-            for r, a in some:
+        def place_scales(e):
+            for a in range(PASSES):
                 nc.sync.dma_start(
-                    out=v_scales[h][SCALE_ROWS * a + r : P : QUADRANT, :].bitcast(I32),
-                    in_=picked_scales[SCALE_ROWS * a + BLOCK * r : P : QUADRANT, h * HALF : (h + 1) * HALF].bitcast(I32),
+                    out=v_scales[PASS_ROW * a + 2 + e : P : QUADRANT, :].bitcast(I32),
+                    in_=picked_scales[QUADRANT // 2 + PASS_ROW * a + e : P : QUADRANT, :].bitcast(I32),
                 )
 
-        place_scales(0, moves[:3])
+        place_scales(0)
         w_raw.append(late.tile([P, PACK, M], F32, name="w_raw1", offset=0, align_bytes=64))
         load_w(1, w_raw[1])
-        place_scales(0, moves[3:])
+        place_scales(1)
 
         gT_rows = gT.rearrange("(h p u) c -> h u p c", p=P, u=PAIR)
         out_rows = out.rearrange("(h p u) j -> h p (u j)", p=P, u=PAIR)
@@ -111,8 +109,6 @@ def tile_list_tabgate_bias_kernel(tc, tab_words, tab_scales, w, gT, b, offs, out
             gates = late.tile([P, T], F32, name="gate_table%d" % t, offset=(2 * t + 1) * WINDOW // 2, align_bytes=64)
             nc.sync.dma_start(out=gates[:], in_=gT_rows[t // PAIR, t % PAIR])
             gate_table.append(gates)
-            if t == 0:
-                place_scales(1, moves)
 
         w_mx = [[], []]
 
@@ -159,34 +155,23 @@ def tile_list_tabgate_bias_kernel(tc, tab_words, tab_scales, w, gT, b, offs, out
         store_ends = [2 * S, 3 * S] + [3 * S + cut for cut in LAST_CUTS] + [4 * S]
         stored = 0
         biased = [held.tile([P, S], F32, name="biased%d" % t) for t in range(N_TILES)]
-        turns = [(t0 + u, h0) for t0 in range(0, N_TILES, PAIR) for h0 in range(0, S, HALF) for u in range(PAIR)]
-        for i, (t, h0) in enumerate(turns):
-            acc = {}
-            for k, j0 in enumerate(range(h0, h0 + HALF, BANK)):
-                acc[j0] = psum.tile([P, BANK], F32, name="acc%d" % ((HALF // BANK * i + k) % BANKS))
-            steps = [(a, j0) for a in range(PASSES) for j0 in acc]
-            if t == 0 and h0 > 0:
-                steps = [(a, j0) for j0 in acc for a in range(PASSES)]
-            for a, j0 in steps:
+        for i, (t, j0) in enumerate((t, j0) for t in range(N_TILES) for j0 in range(0, S, BANK)):
+            acc = psum.tile([P, BANK], F32, name="acc%d" % (i % BANKS))
+            for a in range(PASSES):
                 nc.tensor.matmul_mx(
-                    out=acc[j0][:],
+                    out=acc[:],
                     lhsT=w_mx[a][t][0].bitcast(FP8X4),
                     lhsT_scale=w_mx[a][t][1],
                     rhs=v_words[a][j0 // BANK].bitcast(FP8X4),
-                    rhs_scale=v_scales[h0 // HALF][SCALE_ROWS * a : P, j0 - h0 : j0 - h0 + BANK],
+                    rhs_scale=v_scales[PASS_ROW * a : P, j0 : j0 + BANK],
                     start=(a == 0),
                     stop=(a == PASSES - 1),
                 )
-            for j0 in acc:
-                nc.scalar.activation(
-                    out=biased[t][:, j0 : j0 + BANK], in_=acc[j0][:], func=IDENTITY, bias=bias[:, t : t + 1]
-                )
+            nc.scalar.activation(out=biased[t][:, j0 : j0 + BANK], in_=acc[:], func=IDENTITY, bias=bias[:, t : t + 1])
 
         for t in range(N_TILES):
             if t == 0:
-                cuts = list(range(0, S + 1, BANK))
-            elif t == 1:
-                cuts = [0, HALF, S]
+                cuts = [0, BANK, S]
             elif t == N_TILES - 1:
                 cuts = [0] + LAST_CUTS + [S]
             else:

@@ -155,23 +155,30 @@ def tile_list_tabgate_bias_kernel(tc, tab_words, tab_scales, w, gT, b, offs, out
         store_ends = [2 * S, 3 * S] + [3 * S + cut for cut in LAST_CUTS] + [4 * S]
         stored = 0
         biased = [held.tile([P, S], F32, name="biased%d" % t) for t in range(N_TILES)]
-        for i, (t, j0) in enumerate((t, j0) for t in range(N_TILES) for j0 in range(0, S, BANK)):
-            acc = psum.tile([P, BANK], F32, name="acc%d" % (i % BANKS))
+        turns = [(t, h0) for t in range(N_TILES) for h0 in range(0, S, HALF)]
+        for i, (t, h0) in enumerate(turns):
+            acc = {}
+            for k, j0 in enumerate(range(h0, h0 + HALF, BANK)):
+                acc[j0] = psum.tile([P, BANK], F32, name="acc%d" % ((HALF // BANK * i + k) % BANKS))
             for a in range(PASSES):
-                nc.tensor.matmul_mx(
-                    out=acc[:],
-                    lhsT=w_mx[a][t][0].bitcast(FP8X4),
-                    lhsT_scale=w_mx[a][t][1],
-                    rhs=v_words[a][j0 // BANK].bitcast(FP8X4),
-                    rhs_scale=v_scales[PASS_ROW * a : P, j0 : j0 + BANK],
-                    start=(a == 0),
-                    stop=(a == PASSES - 1),
+                for j0 in acc:
+                    nc.tensor.matmul_mx(
+                        out=acc[j0][:],
+                        lhsT=w_mx[a][t][0].bitcast(FP8X4),
+                        lhsT_scale=w_mx[a][t][1],
+                        rhs=v_words[a][j0 // BANK].bitcast(FP8X4),
+                        rhs_scale=v_scales[PASS_ROW * a : P, j0 : j0 + BANK],
+                        start=(a == 0),
+                        stop=(a == PASSES - 1),
+                    )
+            for j0 in acc:
+                nc.scalar.activation(
+                    out=biased[t][:, j0 : j0 + BANK], in_=acc[j0][:], func=IDENTITY, bias=bias[:, t : t + 1]
                 )
-            nc.scalar.activation(out=biased[t][:, j0 : j0 + BANK], in_=acc[:], func=IDENTITY, bias=bias[:, t : t + 1])
 
         for t in range(N_TILES):
             if t == 0:
-                cuts = [0, BANK, S]
+                cuts = [0, BANK, HALF, S]
             elif t == N_TILES - 1:
                 cuts = [0] + LAST_CUTS + [S]
             else:

@@ -26,7 +26,8 @@ BANK = 512
 HALF = S // 2
 LIST_ROWS = 16
 QUADRANT = 32
-PASS_ROW = 8
+SCALE_ROWS = 4
+BLOCK = 8
 HEAD = 768
 BANKS = 3
 WINDOW = 4 * T
@@ -54,9 +55,8 @@ def tile_list_tabgate_bias_kernel(tc, tab_words, tab_scales, w, gT, b, offs, out
         nc.vector.memset(scale_table[:].bitcast(I32), 0)
         word_table = [late.tile([P, T], I32, name="word_table0", offset=2 * WINDOW, align_bytes=64)]
         load_words(0, word_table[0], 0, HEAD)
-        by_parity = tab_scales.bitcast(I32).rearrange("a (u e) c -> e u a c", e=2)
-        for e in range(2):
-            nc.sync.dma_start(out=scale_table[e:P:PASS_ROW, :].bitcast(I32), in_=by_parity[e])
+        for a in range(PASSES):
+            nc.sync.dma_start(out=scale_table[SCALE_ROWS * a : P : BLOCK, :].bitcast(I32), in_=tab_scales[a].bitcast(I32))
         load_words(0, word_table[0], HEAD, T)
 
         bias_row = held.tile([P, M], F32, name="bias_row")
@@ -81,26 +81,29 @@ def tile_list_tabgate_bias_kernel(tc, tab_words, tab_scales, w, gT, b, offs, out
         load_words(1, word_table[1], 0, T)
 
         picked_scales = late.tile([P, S], U8, name="picked_scales", offset=9 * WINDOW // 2 - S, align_bytes=64)
-        parts = [(0, HALF), (HALF, S)]
+        parts = [(0, S - BANK), (S - BANK, S)]
         for j0, j1 in parts:
             nc.vector.tensor_copy(picked_scales[:, j0:j1], scale_table[:].indirect(entries(j0, j1)))
-        v_scales = held.tile([P, S], U8, name="v_scales", align_bytes=64)
-        for j0, j1 in parts:
-            nc.vector.tensor_copy(v_scales[:, j0:j1].bitcast(I32), picked_scales[:, j0:j1].bitcast(I32))
+        v_scales = [held.tile([P, j1 - j0], U8, name="v_scales%d" % j0, align_bytes=64) for j0, j1 in parts]
+        for part, (j0, j1) in zip(v_scales, parts):
+            nc.vector.tensor_copy(part[:].bitcast(I32), picked_scales[:, j0:j1].bitcast(I32))
         first_words = held.tile([P, S], U32, name="first_words", align_bytes=64)
         nc.vector.tensor_copy(first_words[:], word_table[0][:].bitcast(U32).indirect(offsets[:]))
 
-        def place_scales(e):
-            for a in range(PASSES):
+        moves = [(r, a) for r in range(1, SCALE_ROWS) for a in range(PASSES)]
+
+        def place_scales(i, some):
+            j0, j1 = parts[i]
+            for r, a in some:
                 nc.sync.dma_start(
-                    out=v_scales[PASS_ROW * a + 2 + e : P : QUADRANT, :].bitcast(I32),
-                    in_=picked_scales[QUADRANT // 2 + PASS_ROW * a + e : P : QUADRANT, :].bitcast(I32),
+                    out=v_scales[i][SCALE_ROWS * a + r : P : QUADRANT, :].bitcast(I32),
+                    in_=picked_scales[SCALE_ROWS * a + BLOCK * r : P : QUADRANT, j0:j1].bitcast(I32),
                 )
 
-        place_scales(0)
+        place_scales(0, moves[:3])
         w_raw.append(late.tile([P, PACK, M], F32, name="w_raw1", offset=0, align_bytes=64))
         load_w(1, w_raw[1])
-        place_scales(1)
+        place_scales(0, moves[3:])
 
         gT_rows = gT.rearrange("(h p u) c -> h u p c", p=P, u=PAIR)
         out_rows = out.rearrange("(h p u) j -> h p (u j)", p=P, u=PAIR)
@@ -109,6 +112,8 @@ def tile_list_tabgate_bias_kernel(tc, tab_words, tab_scales, w, gT, b, offs, out
             gates = late.tile([P, T], F32, name="gate_table%d" % t, offset=(2 * t + 1) * WINDOW // 2, align_bytes=64)
             nc.sync.dma_start(out=gates[:], in_=gT_rows[t // PAIR, t % PAIR])
             gate_table.append(gates)
+            if t == 0:
+                place_scales(1, moves)
 
         w_mx = [[], []]
 
@@ -155,30 +160,39 @@ def tile_list_tabgate_bias_kernel(tc, tab_words, tab_scales, w, gT, b, offs, out
         store_ends = [2 * S, 3 * S] + [3 * S + cut for cut in LAST_CUTS] + [4 * S]
         stored = 0
         biased = [held.tile([P, S], F32, name="biased%d" % t) for t in range(N_TILES)]
-        turns = [(t, h0) for t in range(N_TILES) for h0 in range(0, S, HALF)]
-        for i, (t, h0) in enumerate(turns):
-            acc = {}
-            for k, j0 in enumerate(range(h0, h0 + HALF, BANK)):
-                acc[j0] = psum.tile([P, BANK], F32, name="acc%d" % ((HALF // BANK * i + k) % BANKS))
+        early = [(t, j0) for t in range(N_TILES) for j0 in range(0, S - BANK, BANK)]
+        last = [(t, S - BANK) for t in range(N_TILES)]
+        units = early[:5] + last[:BANKS] + early[5:] + last[BANKS:]
+        v_planes = [v_scales[0][:, j0 : j0 + BANK] for j0 in range(0, S - BANK, BANK)] + [v_scales[1][:]]
+        acc = {}
+
+        def product(i, a):
+            t, j0 = units[i]
+            if a == 0:
+                acc[i] = psum.tile([P, BANK], F32, name="acc%d" % (i % BANKS))
+            nc.tensor.matmul_mx(
+                out=acc[i][:],
+                lhsT=w_mx[a][t][0].bitcast(FP8X4),
+                lhsT_scale=w_mx[a][t][1],
+                rhs=v_words[a][j0 // BANK].bitcast(FP8X4),
+                rhs_scale=v_planes[j0 // BANK][SCALE_ROWS * a : P, :],
+                start=(a == 0),
+                stop=(a == PASSES - 1),
+            )
+
+        for i0 in range(0, len(units), 2):
             for a in range(PASSES):
-                for j0 in acc:
-                    nc.tensor.matmul_mx(
-                        out=acc[j0][:],
-                        lhsT=w_mx[a][t][0].bitcast(FP8X4),
-                        lhsT_scale=w_mx[a][t][1],
-                        rhs=v_words[a][j0 // BANK].bitcast(FP8X4),
-                        rhs_scale=v_scales[PASS_ROW * a : P, j0 : j0 + BANK],
-                        start=(a == 0),
-                        stop=(a == PASSES - 1),
-                    )
-            for j0 in acc:
+                for i in (i0, i0 + 1):
+                    product(i, a)
+            for i in (i0, i0 + 1):
+                t, j0 = units[i]
                 nc.scalar.activation(
-                    out=biased[t][:, j0 : j0 + BANK], in_=acc[j0][:], func=IDENTITY, bias=bias[:, t : t + 1]
+                    out=biased[t][:, j0 : j0 + BANK], in_=acc[i][:], func=IDENTITY, bias=bias[:, t : t + 1]
                 )
 
         for t in range(N_TILES):
             if t == 0:
-                cuts = [0, BANK, HALF, S]
+                cuts = list(range(0, S + 1, BANK))
             elif t == N_TILES - 1:
                 cuts = [0] + LAST_CUTS + [S]
             else:

@@ -120,20 +120,20 @@ def tile_list_tabgate_bias_kernel(tc, tab_words, tab_scales, w, gT, b, offs, out
         def quantise_w(a, t0, t1):
             width = (t1 - t0) * P
             grouped = held.tile([P, width * PACK], BF16, name="w_grouped%d_%d" % (a, t0), align_bytes=64)
-            by_feature = w_raw[a][:].rearrange("p i (h m u) -> p h m u i", m=P, u=PAIR)
+            by_feature = w_raw[a][:].rearrange("p i (h g e u) -> p h g i e u", e=2, u=PAIR, h=N_TILES // PAIR)
             t = t0
             while t < t1:
                 h, u = divmod(t, PAIR)
-                halves = (t1 - t) // PAIR if u == 0 else 0
-                count = halves * PAIR if halves else 1
+                count = PAIR if u == 0 and t1 - t >= PAIR else 1
                 part = grouped[:, (t - t0) * P * PACK : (t - t0 + count) * P * PACK]
-                if halves:
+                if count == PAIR:
                     nc.scalar.copy(
-                        out=part.rearrange("p (h u m i) -> p h m u i", u=PAIR, m=P, i=PACK),
-                        in_=by_feature[:, h : h + halves],
+                        out=part.rearrange("p (u g e i) -> p g i e u", u=PAIR, e=2, i=PACK), in_=by_feature[:, h]
                     )
                 else:
-                    nc.scalar.copy(out=part.rearrange("p (m i) -> p m i", i=PACK), in_=by_feature[:, h, :, u, :])
+                    nc.scalar.copy(
+                        out=part.rearrange("p (g e i) -> p g i e", e=2, i=PACK), in_=by_feature[:, h, :, :, :, u]
+                    )
                 t = t + count
             codes = held.tile([P, width], U32, name="w_codes%d_%d" % (a, t0), align_bytes=64)
             scales = held.tile([P, width], U8, name="w_scales%d_%d" % (a, t0), align_bytes=64)
@@ -148,9 +148,9 @@ def tile_list_tabgate_bias_kernel(tc, tab_words, tab_scales, w, gT, b, offs, out
         second_words = held.tile([P, S - BANK], U32, name="second_words", align_bytes=64)
         nc.vector.tensor_copy(second_words[:], second_window.indirect(entries(0, S - BANK)))
         quantise_w(1, 0, 1)
-        last_words = held.tile([P, BANK], U32, name="w_grouped1_0", align_bytes=64)
-        nc.vector.tensor_copy(last_words[:], second_window.indirect(entries(S - BANK, S)))
         quantise_w(1, 1, N_TILES)
+        last_words = late.tile([P, BANK], U32, name="last_words", offset=0, align_bytes=64)
+        nc.vector.tensor_copy(last_words[:], second_window.indirect(entries(S - BANK, S)))
         v_words = [
             [first_words[:, j0 : j0 + BANK] for j0 in range(0, S, BANK)],
             [second_words[:, j0 : j0 + BANK] for j0 in range(0, S - BANK, BANK)] + [last_words[:]],

from contextlib import ExitStack

import concourse.mybir as mybir
from concourse.masks import make_identity

K, M, T, S = 1024, 512, 4096, 2048
FLOPS = 2 * K * M * S

F32 = mybir.dt.float32
BF16 = mybir.dt.bfloat16
I32 = mybir.dt.int32
U32 = mybir.dt.uint32
U16 = mybir.dt.uint16
U8 = mybir.dt.uint8
FP8X4 = mybir.dt.float8_e4m3fn_x4
IDENTITY = mybir.ActivationFunctionType.Identity
MULT = mybir.AluOpType.mult

P = 128
PACK = 4
K_PASS = P * PACK
PASSES = K // K_PASS
N_TILES = M // P
PAIR = 2
BANK = 512
HALF = S // 2
LIST_ROWS = 16
QUADRANT = 32
SCALE_ROWS = 4
BLOCK = 8
HEAD = 768
BANKS = 3
WINDOW = 4 * T
LAST_CUTS = [1120, 1664, 1920]


def tile_list_tabgate_bias_kernel(tc, tab_words, tab_scales, w, gT, b, offs, out):
    nc = tc.nc
    with ExitStack() as ctx:
        held = ctx.enter_context(tc.tile_pool(name="held", bufs=1))
        late = ctx.enter_context(tc.tile_pool(name="late", bufs=1))
        psum = ctx.enter_context(tc.psum_pool(name="psum", bufs=1))
        turn = ctx.enter_context(tc.psum_pool(name="turn", bufs=1))

        offsets = held.tile([P, S // LIST_ROWS], U16, name="offsets")
        nc.sync.dma_start(offsets[:], offs)

        def entries(j0, j1):
            return offsets[:, j0 // LIST_ROWS : j1 // LIST_ROWS]

        def load_words(a, words, c0, c1):
            nc.sync.dma_start(out=words[:, c0:c1], in_=tab_words[a].rearrange("p c i -> p (c i)").bitcast(I32)[:, c0:c1])

        scale_table = late.tile([P, T], U8, name="scale_table", offset=WINDOW // 2 - T // 2, align_bytes=64)
        nc.vector.memset(scale_table[:].bitcast(I32), 0)
        word_table = [late.tile([P, T], I32, name="word_table0", offset=2 * WINDOW, align_bytes=64)]
        load_words(0, word_table[0], 0, HEAD)
        for a in range(PASSES):
            nc.sync.dma_start(out=scale_table[SCALE_ROWS * a : P : BLOCK, :].bitcast(I32), in_=tab_scales[a].bitcast(I32))
        load_words(0, word_table[0], HEAD, T)

        bias_row = held.tile([P, M], F32, name="bias_row")
        nc.vector.memset(bias_row[:], 0.0)
        nc.sync.dma_start(out=bias_row[0:1, :], in_=b.rearrange("(o n) -> o n", o=1))
        identity = held.tile([P, P], F32, name="identity")
        nc.vector.memset(identity[:], 0.0)
        make_identity(nc, identity[:], nomemset=True)
        turned = turn.tile([P, N_TILES, P], F32, name="turned")
        for t in range(N_TILES):
            h, u = divmod(t, PAIR)
            nc.tensor.transpose(turned[:, t, :], bias_row[:, h * PAIR * P + u : (h + 1) * PAIR * P : PAIR], identity[:])

        def load_w(a, raw):
            nc.sync.dma_start(
                out=raw[:], in_=w[a * K_PASS : (a + 1) * K_PASS, :].rearrange("(p i) n -> p i n", i=PACK)
            )

        w_raw = [held.tile([P, PACK, M], F32, name="w_raw0")]
        load_w(0, w_raw[0])
        word_table.append(held.tile([P, T], I32, name="word_table1", align_bytes=64))
        load_words(1, word_table[1], 0, T)

        picked_scales = late.tile([P, S], U8, name="picked_scales", offset=9 * WINDOW // 2 - S, align_bytes=64)
        parts = [(0, S - BANK), (S - BANK, S)]
        for j0, j1 in parts:
            nc.vector.tensor_copy(picked_scales[:, j0:j1], scale_table[:].indirect(entries(j0, j1)))
        v_scales = [held.tile([P, j1 - j0], U8, name="v_scales%d" % j0, align_bytes=64) for j0, j1 in parts]
        for part, (j0, j1) in zip(v_scales, parts):
            nc.vector.tensor_copy(part[:].bitcast(I32), picked_scales[:, j0:j1].bitcast(I32))
        first_words = held.tile([P, S], U32, name="first_words", align_bytes=64)
        nc.vector.tensor_copy(first_words[:], word_table[0][:].bitcast(U32).indirect(offsets[:]))

        moves = [(r, a) for r in range(1, SCALE_ROWS) for a in range(PASSES)]

        def place_scales(i, some):
            j0, j1 = parts[i]
            for r, a in some:
                nc.sync.dma_start(
                    out=v_scales[i][SCALE_ROWS * a + r : P : QUADRANT, :].bitcast(I32),
                    in_=picked_scales[SCALE_ROWS * a + BLOCK * r : P : QUADRANT, j0:j1].bitcast(I32),
                )

        place_scales(0, moves[:3])
        w_raw.append(late.tile([P, PACK, M], F32, name="w_raw1", offset=0, align_bytes=64))
        load_w(1, w_raw[1])
        place_scales(0, moves[3:])

        gT_rows = gT.rearrange("(h p u) c -> h u p c", p=P, u=PAIR)
        out_rows = out.rearrange("(h p u) j -> h p (u j)", p=P, u=PAIR)
        gate_table = []
        for t in range(N_TILES):
            gates = late.tile([P, T], F32, name="gate_table%d" % t, offset=(2 * t + 1) * WINDOW // 2, align_bytes=64)
            nc.sync.dma_start(out=gates[:], in_=gT_rows[t // PAIR, t % PAIR])
            gate_table.append(gates)
            if t == 0:
                place_scales(1, moves)

        w_mx = [[], []]

        def quantise_w(a, t0, t1):
            width = (t1 - t0) * P
            grouped = held.tile([P, width * PACK], BF16, name="w_grouped%d_%d" % (a, t0), align_bytes=64)
            by_feature = w_raw[a][:].rearrange("p i (h g e u) -> p h g i e u", e=2, u=PAIR, h=N_TILES // PAIR)
            t = t0
            while t < t1:
                h, u = divmod(t, PAIR)
                count = PAIR if u == 0 and t1 - t >= PAIR else 1
                part = grouped[:, (t - t0) * P * PACK : (t - t0 + count) * P * PACK]
                if count == PAIR:
                    nc.scalar.copy(
                        out=part.rearrange("p (u g e i) -> p g i e u", u=PAIR, e=2, i=PACK), in_=by_feature[:, h]
                    )
                else:
                    nc.scalar.copy(
                        out=part.rearrange("p (g e i) -> p g i e", e=2, i=PACK), in_=by_feature[:, h, :, :, :, u]
                    )
                t = t + count
            codes = held.tile([P, width], U32, name="w_codes%d_%d" % (a, t0), align_bytes=64)
            scales = held.tile([P, width], U8, name="w_scales%d_%d" % (a, t0), align_bytes=64)
            nc.vector.quantize_mx(out=codes[:].bitcast(FP8X4), scales=scales[:], in_=grouped[:])
            for c0 in range(0, width, P):
                w_mx[a].append((codes[:, c0 : c0 + P], scales[:, c0 : c0 + P]))

        quantise_w(0, 0, N_TILES)
        bias = held.tile([P, N_TILES], F32, name="w_raw0")
        nc.scalar.copy(out=bias[:], in_=turned[:, :, 0])
        second_window = word_table[1][:].bitcast(U32)
        second_words = held.tile([P, S - BANK], U32, name="second_words", align_bytes=64)
        nc.vector.tensor_copy(second_words[:], second_window.indirect(entries(0, S - BANK)))
        quantise_w(1, 0, 1)
        quantise_w(1, 1, N_TILES)
        last_words = late.tile([P, BANK], U32, name="last_words", offset=0, align_bytes=64)
        nc.vector.tensor_copy(last_words[:], second_window.indirect(entries(S - BANK, S)))
        v_words = [
            [first_words[:, j0 : j0 + BANK] for j0 in range(0, S, BANK)],
            [second_words[:, j0 : j0 + BANK] for j0 in range(0, S - BANK, BANK)] + [last_words[:]],
        ]

        result = held.tile([P, N_TILES * S], F32, name="result")
        store_ends = [2 * S, 3 * S] + [3 * S + cut for cut in LAST_CUTS] + [4 * S]
        stored = 0
        biased = [held.tile([P, S], F32, name="biased%d" % t) for t in range(N_TILES)]
        early = [(t, j0) for t in range(N_TILES) for j0 in range(0, S - BANK, BANK)]
        last = [(t, S - BANK) for t in range(N_TILES)]
        units = early[:5] + last[:BANKS] + early[5:] + last[BANKS:]
        v_planes = [v_scales[0][:, j0 : j0 + BANK] for j0 in range(0, S - BANK, BANK)] + [v_scales[1][:]]
        acc = {}

        def product(i, a):
            t, j0 = units[i]
            if a == 0:
                acc[i] = psum.tile([P, BANK], F32, name="acc%d" % (i % BANKS))
            nc.tensor.matmul_mx(
                out=acc[i][:],
                lhsT=w_mx[a][t][0].bitcast(FP8X4),
                lhsT_scale=w_mx[a][t][1],
                rhs=v_words[a][j0 // BANK].bitcast(FP8X4),
                rhs_scale=v_planes[j0 // BANK][SCALE_ROWS * a : P, :],
                start=(a == 0),
                stop=(a == PASSES - 1),
            )

        for i0 in range(0, len(units), 2):
            for a in range(PASSES):
                for i in (i0, i0 + 1):
                    product(i, a)
            for i in (i0, i0 + 1):
                t, j0 = units[i]
                nc.scalar.activation(
                    out=biased[t][:, j0 : j0 + BANK], in_=acc[i][:], func=IDENTITY, bias=bias[:, t : t + 1]
                )

        for t in range(N_TILES):
            if t == 0:
                cuts = list(range(0, S + 1, BANK))
            elif t == N_TILES - 1:
                cuts = [0] + LAST_CUTS + [S]
            else:
                cuts = [0, S]
            for j0, j1 in zip(cuts, cuts[1:]):
                done = t * S + j1
                nc.vector.tensor_tensor(
                    result[:, t * S + j0 : done],
                    gate_table[t][:].indirect(entries(j0, j1)),
                    biased[t][:, j0:j1],
                    MULT,
                )
                if done in store_ends:
                    base = t // PAIR * PAIR * S
                    nc.sync.dma_start(out=out_rows[t // PAIR][:, stored - base : done - base], in_=result[:, stored:done])
                    stored = done
